import numpy as np, ml_dtypes
CORES = [23,119,17,113]
N = 4
import mx_ref
BF = ml_dtypes.bfloat16
def gcols(t, e):
    v = np.concatenate([t.reshape(8, 16, -1, 4), np.zeros((8, 16, 1, 4), BF)], axis=2)
    return np.ascontiguousarray(np.stack([v[g][:, e[g]] for g in range(8)])).reshape(128, -1)
def pick(q, e):
    c = np.concatenate([q[0].reshape(128, -1, 4), np.zeros((128, 1, 4), np.uint8)], axis=1); s = np.concatenate([q[1], np.ones((16, 1), np.uint8)], axis=1)
    return (np.ascontiguousarray(c[:, e].reshape(128, -1)), np.ascontiguousarray(s[:, e]))
def join(*qs):
    return (np.concatenate([q[0] for q in qs], axis=1), np.concatenate([q[1] for q in qs], axis=1))
def put(q, e, v):
    c, s = q[0].reshape(128, -1, 4).copy(), q[1].copy(); c[:, e] = v[0].reshape(128, -1, 4); s[:, e] = v[1]
    return (c.reshape(128, -1), s)
def pk(c, s):
    return (np.ascontiguousarray(c), mx_ref.live(s))
def emit(q):
    return q[0], q[1]
def packed(v, rng):
    q = [mx_ref.quantize(np.ascontiguousarray(v[r])) for r in range(N)]
    return np.stack([a for a, b in q]), np.stack([mx_ref.plane(b, rng) for a, b in q])
def values_of_codes():
    e, c = np.zeros((128, 128, 4), np.float32), np.zeros((128, 2, 4), np.uint8)
    e[np.arange(128), np.arange(128), 0] = 1
    c[:127, :, 0] = np.arange(256).reshape(2, 128).T[:127]
    return mx_ref.matmul(mx_ref.quantize(e.reshape(128, 512).astype(BF)), (c.reshape(128, 8), np.full((16, 2), 127, np.uint8))).T.reshape(-1).astype(np.float64)
CODE_VALUE, SCALE_VALUE = values_of_codes(), 2.0 ** (np.arange(256) - 127.0)
def decode(q):
    return (CODE_VALUE[q[0]].reshape(16, 8, -1, 4) * SCALE_VALUE[q[1]][:, None, :, None] + 0.0).reshape(128, -1).astype(np.float32)
def f(rng, *shape):
    return mx_ref.flush((rng.standard_normal(shape, dtype=np.float32) * np.exp2(rng.integers(-2, 3, shape[:-1] + (1,)))).astype(BF))
def wide(rng, *shape, cols=0):
    v = rng.standard_normal(shape, dtype=np.float32) * np.exp2(rng.integers(-12, 13, shape)).astype(np.float32)
    if cols: v *= np.repeat(np.exp2(rng.integers(-cols, cols + 1, shape[:-2] + (1, shape[-1] // 4))) * (rng.random(shape[:-2] + (1, shape[-1] // 4)) > 0.0625), 4, axis=-1).astype(np.float32)
    return mx_ref.flush(v.astype(BF))
C, L, K = 400, 20, 160
MASKS = [1, 2, 3]
def big(v):
    v = v.astype(np.float32)
    v[np.abs(v) < np.float32(2.0 ** -16)] = 0
    return v.astype(BF)
def numbers_of(rng):
    return {"x": big(f(rng, N, 128, 4 * C)), "u": np.array(f(rng, N, 128, 512)), "v": np.array(f(rng, N, 128, 512))}
def layers(rng, still=[]):
    w = big(f(rng, N, 128, 2048)).reshape(N, 8, 16, 4, 8, 16, 4)
    for i in still:
        w[:, :, i] = 0
        w[:, :, :, :, :, i] = 0
    return w
def weights(rng, w):
    c, s = packed(np.ascontiguousarray(w).reshape(N, 128, 2048), rng)
    return {"wc": c, "ws": s}
def bare(u):
    u = u.reshape(N, 128, 128, 4)
    u[:, :, ::16] = 0
    u[:, :, 1::16] = 0
    return u
def back(x):
    return np.ascontiguousarray(x).astype(np.float32).reshape(N, 128, 4 * C).astype(BF)
def setup_inputs(rng):
    return {**numbers_of(rng), **weights(rng, layers(rng))}
def setup_inputs_ties(rng):
    d = numbers_of(rng)
    x = d["x"].astype(np.float32).reshape(N, 8, 16, C, 4)
    x[:, :, 0] = 0
    for b in range(2): x[:, :, 0, :, b] = np.minimum(rng.integers(0, 3, (N, 8, L, L)), rng.integers(0, 3, (N, 8, L, 1))).reshape(N, 8, C)
    u = bare(d["u"])
    o = rng.permutation(N)
    for r in range(N):
        k = 0.0 if r == o[0] else -1.0 if r == o[1] else 1.0
        for h in range(0, 128, 16):
            u[r, h, h, 0] = k
            u[r, h, h + 1, 1] = k
    return {"x": back(x), "u": u.reshape(N, 128, 512), "v": d["v"], **weights(rng, layers(rng, [0]))}
def setup_inputs_near(rng):
    d = numbers_of(rng)
    x = d["x"].astype(np.float32).reshape(N, 8, 16, C, 4)
    u = bare(d["u"])
    x[:, :, :2] = 0
    x[:, :, 8:] = 0
    o = rng.permutation(8) % 4
    for g in range(8):
        h, a = 16 * g, 2.0 ** -30 if o[g] >= 2 else 1.0
        if o[g] == 3:
            x[:, g, 10:12, :, 0] = 2.0 ** -29 * (1.0 + 0.125 * rng.integers(0, 6, (N, 2, C)))
            u[:, h + 10, h, 0] = -a
            u[:, h + 11, h + 1, 0] = -a
            continue
        i = h + 1 if o[g] == 1 else h
        x[:, g, 0, :, 0] = rng.integers(0, 2, (N, 1)) * 2.0 - 1.0
        x[:, g, 8:10] = ((rng.integers(0, 16, (N, 2, C))[..., None] >> np.arange(4)) & 1) * np.exp2(np.arange(4) - 23.0)
        x[:, g, 11, :, 0] = 2.0 ** -10
        u[:, h, i, 0] = a
        u[:, h + 11, i, 0] = a
        u[:, h + 8, h] = a
        u[:, h + 9, h + 1] = a
        if o[g] == 1: x[np.arange(N), g, 0, rng.integers(0, C, N), 0] = -2.0 ** 29
        else:
            for r in range(N):
                k = rng.permutation(L)
                x[r, g, 0, L * k[0]:L * k[0] + L, 0] = -2.0 ** 29
                x[r, g, 0, L * k[1] + rng.integers(0, L), 0] = 2.0 ** 29 * (rng.integers(0, 2) * 2.0 - 1.0)
    return {"x": back(x), "u": u.reshape(N, 128, 512), "v": d["v"], **weights(rng, layers(rng, [0, 1] + [8 + i for i in range(8)]))}
def setup_inputs_huge(rng):
    d = numbers_of(rng)
    x = -2.0 ** 30 * np.where(rng.random((N, 8, 16, C, 4)) < rng.random((N, 8, 1, C, 1)), 0.9375, 0.875)
    u = bare(d["u"])
    o = rng.permutation(8)
    for g in range(8):
        for b in range(2):
            for h in rng.permutation(8)[:8 if o[g] < 3 else 2]: u[:, 16 * h:16 * h + 16, 16 * g + b] = 2.0 ** 30 if o[g] % 2 == 0 else -2.0 ** 30
    w = np.zeros((N, 128, 4, 128, 4), np.float32)
    i = np.arange(128)
    for b in range(4): w[:, i, b, i, b] = -2
    return {"x": back(x), "u": u.reshape(N, 128, 512), "v": d["v"], **weights(rng, w.astype(BF))}
def setup_inputs_late(rng):
    d = numbers_of(rng)
    x = d["x"].astype(np.float32).reshape(N, 8, 16, C, 4)
    x[:, :, 8:] = (1.125 + 0.25 * rng.integers(0, 4, (N, 8, 8, C, 4))) * np.exp2(rng.integers(-1, 2, (N, 8, 8, C, 4))) * rng.choice([-1.0, 1.0], (N, 8, 8, C, 4))
    x[:, :, 8, :, 2:] = 1.96875 * 2.0 ** 13 * rng.choice([-1.0, 1.0], (8, 1, 1))
    u = bare(d["u"])
    for h in range(0, 128, 16):
        u[:, h, h, 0] = 1.0
        u[:, h, h + 1, 1] = 1.0
    s = MASKS[0]
    none = rng.permutation([r for r in range(N) if r < r ^ s])[:N // 4]
    for r in range(N):
        if min(r, r ^ s) in none: x[r, :, :8] = 0
        else:
            a = np.zeros((8, L, L), np.float32)
            np.put_along_axis(a, rng.integers(0, L, (8, L, 1)), np.exp2(np.argsort(rng.random((8, L, 1)), axis=1).astype(np.float32)), axis=2)
            x[r, :, 0] = 0
            x[r, :, 0, :, 0] = a.reshape(8, C)
            for h in range(0, 128, 16): u[r, h + 9, h + 1, 1] = 0.125
    w = layers(rng)
    w[:, :, 0] = 0
    w[:, :, 8] = 0
    for g in range(8):
        w[:, g, 8, 2:, g, 8, 2] = 16
        w[:, g, 8, 2:, g, 8, 3] = 15
    return {"x": back(x), "u": u.reshape(N, 128, 512), "v": d["v"], **weights(rng, w)}
def setup_inputs_spread(rng):
    d = setup_inputs(rng)
    d["x"] = big(wide(rng, N, 128, 4 * C, cols=6))
    return d
def check_inputs(d):
    b = []
    for k in ("x", "u", "v"):
        a = np.abs(d[k].astype(np.float32))
        if not (np.isfinite(a).all() and ((a == 0) | (a >= 2.0 ** -30) & (a <= 2.0 ** 30)).all()): b.append("a value of " + k)
    none, least, most = [emit(mx_ref.quantize(np.full((128, 16), k, np.float32).astype(BF)))[1][0, 0] for k in (0.0, 2.0 ** -30, 2.0 ** 30)]
    for r in range(N):
        if ((d["wc"][r] == 0x7F) | (d["wc"][r] == 0xFF)).any(): b.append("wc: a code that is no number")
        s = mx_ref.live(d["ws"][r])
        if ((s != none) & ((s < least) | (s > most))).any(): b.append("ws: a scale out of range")
    return b
def reference(x, u, v, wc, ws):
    qu = [mx_ref.quantize(u[r]) for r in range(N)]
    lay = [pk(wc[r], ws[r]) for r in range(N)]
    now = [x[r] for r in range(N)]
    for s in MASKS:
        q = [mx_ref.quantize(now[r]) for r in range(N)]
        t = [decode(q[r]) for r in range(N)]
        score = [mx_ref.matmul(qu[r], q[r]) + np.float32(0.0) for r in range(N)]
        made = []
        for r in range(N):
            d = r ^ s
            both = score[r][::16].reshape(8, L, 1, L) + score[d][1::16].reshape(8, 1, L, L)
            best, middle = np.max(both, axis=3).reshape(8, C), np.argmax(both, axis=3).reshape(8, C)
            e = np.argsort(-best, axis=1, kind="stable")[:, :K]
            m = np.take_along_axis(middle, e, axis=1)
            one = gcols(t[r].astype(BF), e // L * L + m).astype(np.float32)
            two = decode(mx_ref.quantize(gcols(t[d].astype(BF), e % L * L + m)))
            z = mx_ref.quantize(((one + two) * np.float32(0.5)).astype(BF))
            h = np.stack([mx_ref.matmul(pick(lay[r], np.arange(128 * b, 128 * b + 128)), z) * np.float32(0.03125) for b in range(4)], axis=2).reshape(8, 16, K, 4)
            n = t[r].reshape(8, 16, C, 4).copy()
            for g in range(8): n[g][:, e[g]] = n[g][:, e[g]] + h[g]
            made.append(n.reshape(128, 4 * C).astype(BF))
        now = made
    y = np.zeros((N, 128, C), np.float32)
    oc, osc = np.zeros((N, 128, 4 * C), np.uint8), np.zeros((N, 16, C), np.uint8)
    for r in range(N):
        q = mx_ref.quantize(now[r])
        y[r] = mx_ref.matmul(mx_ref.quantize(v[r]), q)
        oc[r], osc[r] = emit(q)
    return {"y": y, "oc": oc, "osc": osc}

@@ -1,0 +1,469 @@
+from concourse.bass import IndirectOffsetOnAxis
+from concourse.mybir import dt, AluOpType, ActivationFunctionType
+
+C, L, K, ROUNDS = 400, 20, 160, 3
+MASKS = [1, 2, 3]
+NP = 25
+NB = 12
+SL = 13
+NS = 11
+CW = 80
+RB = 16.0 * NB - 1
+WW = 576
+
+F32, BF, I32, U16, X4, U8 = "float32", "bfloat16", "int32", "uint16", "float8_e4m3fn_x4", "uint8"
+SCRATCH = {"ps": ("psum", [128, 4096], F32), "tbl": ("dram", [8, C], F32)}
+for _d, _l in (
+    (BF, dict(xin=4 * C, uin=512, vin=512, et=2048, qrow=C, dmask=C, smask=C, r20m=512, r16=832, r13=SL * CW, lt=512, mid=512,
+              dif=C, eqd=C, eqs=C, ged=C, ges=C, wv=SL * C, wo=SL * 432, sg=SL * 192, junk=NP * 192, ctr=832, cseg=832,
+              tt=4 * C, w32=4 * WW, tb=4 * C, ah=4 * K, te=4 * K, zt=4 * K, xt=4 * C)),
+    (F32, dict(pc=12, km=12, jrow=128, n16=32, nn=32, ca=96, cc=256, cl=256, r20a=512, sel1=C, sel1h=200, sel0=C, sel0h=200,
+               a0=100, aexp=512, sums=512, rmax=512, brep=800, btr=800, row=C, rowd=C, piv=C, acc=32, acc2=32, pp=96, nrk=32,
+               vblk=64, vcb=32, vrep=C, vrow=C, ew=C + 16, etr=352, lf=32, lh=48, xa=96, yo=C,
+               out0=100, out1=100, out2=100, land0=100, land1=100, land2=100)),
+    (I32, dict(pi=1, pb=8, ui=16, cb=96, ri=76, li=16, lj=32, lg=32, lb=16)),
+    (U16, dict(uo=16, co=160, ro=76, so=4, rko=32, la=16, lo=16, le=16, xo=32)),
+    (X4, dict(wq=512, uq=128, urq=256, vq=128, eq=512, zq=K, xq0=C, xq1=C, xq2=C, xq3=C, tq0=C, tq1=C, tq2=C, lq0=C, lq1=C, lq2=C)),
+    (U8, dict(wsc=512, usc=128, ursc=256, vsc=128, esc=512, zsc=K, xs0=C, xs1=C, xs2=C, xs3=C, ts0=C, ts1=C, ts2=C, ls0=C, ls1=C, ls2=C)),
+):
+    for _n, _w in _l.items():
+        SCRATCH[_n] = ("sbuf", [128, _w], _d)
+SEMAPHORES = (["cv", "cs", "ct", "cg", "sent", "rows"] + ["d%d" % _i for _i in range(20)]
+              + ["arrs%d" % _r for _r in range(ROUNDS)] + ["arrc%d" % _r for _r in range(ROUNDS)])
+
+A = AluOpType
+ACT = ActivationFunctionType
+
+
+def rank_program(g, core, T, topo):
+    rank = T.rank_of(core)
+    if rank is None:
+        return
+    V, S, PE = g.vector, g.scalar, g.tensor
+    queue = {"v": V, "s": S, "t": PE, "g": g, "y": g.sync}
+    own = {"v": "cv", "s": "cs", "t": "ct", "g": "cg"}
+    count = {}
+    waited = {e: {} for e in queue}
+    writer, readers = {}, {}
+    ndma = [0]
+
+    def need(e, deps):
+        top = {}
+        for s, n in deps:
+            top[s] = max(top.get(s, 0), n)
+        for s, n in top.items():
+            if waited[e].get(s, 0) < n:
+                queue[e].wait_ge(T.sem[s], n)
+                waited[e][s] = n
+
+    def order(e, R, W, P):
+        deps = [writer[k] for k in list(R) + list(W) + list(P) if k in writer]
+        for k in W:
+            deps += readers.get(k, [])
+        for k in P:
+            deps += [d for d in readers.get(k, []) if d[0] != own.get(e)]
+        need(e, deps)
+
+    def done(mark, R, W, P):
+        for k in list(R) + list(P):
+            readers.setdefault(k, []).append(mark)
+        for k in W:
+            writer[k] = mark
+            readers[k] = []
+
+    def op(e, call, R=(), W=(), P=()):
+        order(e, R, W, P)
+        s = own[e]
+        call().then_inc(T.sem[s], 1)
+        count[s] = count.get(s, 0) + 1
+        done((s, count[s]), R, W, P)
+
+    def dma(e, out, in_, R=(), W=()):
+        order(e, R, W, ())
+        s = "d%d" % ndma[0]
+        ndma[0] += 1
+        queue[e].dma_start(out, in_).then_inc(T.sem[s], 16)
+        count[s] = 16
+        done((s, 16), R, W, ())
+
+    def engines_of(m):
+        return bin(m).count("1")
+
+    def send(dst, out, in_, sem, m, R):
+        order("g", R, (), ())
+        rid, pid = topo.addr(dst)[:2]
+        g.remote_dma(out, in_, T.sem[sem], T.sem.sent, pid, rid, m)
+        count["sent"] = count.get("sent", 0) + engines_of(m)
+
+    def bank(k, n, a=0):
+        return T.ps[:, 512 * k + a:512 * k + a + n]
+
+    def u8(view):
+        return view.bitcast(dt.uint8)
+
+    def ts(out, in0, s1, s2, o0, o1=None):
+        if o1 is None:
+            return lambda: V.tensor_scalar(out, in0, s1, None, o0)
+        return lambda: V.tensor_scalar(out, in0, s1, s2, o0, o1)
+
+    def tt(out, in0, in1, o):
+        return lambda: V.tensor_tensor(out, in0, in1, o)
+
+    def cp(out, in_):
+        return lambda: V.tensor_copy(out, in_)
+
+    def scan(out, d0, d1, o0, o1):
+        return lambda: V.tensor_tensor_scan(out, d0, d1, 0.0, o0, o1)
+
+    def turn(out, in_):
+        return lambda: V.transpose(out, in_)
+
+    def quant(codes, plane, tile):
+        return lambda: V.quantize_mx(codes, plane, tile)
+
+    def act(out, in_, f, **kw):
+        return lambda: S.activation(out, in_, f, **kw)
+
+    def fill(out, n, c, keys):
+        op("s", act(out, T.r13[:, 0:n], ACT.Identity, scale=0.0, bias=c), R=["ones"], W=keys)
+
+    def iota(out, pattern, base=0, cm=0, small=False):
+        if small:
+            return lambda: g.iota(out, pattern, base, cm, allow_small_or_imprecise_dtypes=True)
+        return lambda: g.iota(out, pattern, base, cm)
+
+    def mm(k, n, lq, ls, rq, rs):
+        return lambda: PE.matmul_mx(bank(k, n), lq, ls, rq, rs, True, True)
+
+    def col(i):
+        return T.pc[:, i:i + 1]
+
+    partners = [T.cores[rank ^ s] for s in MASKS]
+    common = topo.mask(core, partners[0])
+    for d in partners:
+        common &= topo.mask(core, d)
+
+    dma("s", T.uin[:], T.u[:], W=["uin"])
+    dma("y", T.xin[:, 0:800], T.x[:, 0:800], W=["xin0"])
+    dma("s", T.xin[:, 800:1600], T.x[:, 800:1600], W=["xin1"])
+
+    k4, p1, p2, p3 = T.km[:, 0:4], T.pp[:, 0:32], T.pp[:, 32:64], T.pp[:, 64:96]
+    op("g", iota(T.pi[:], [[0, 1]], 0, 1), W=["pi"])
+    op("g", iota(T.jrow[:], [[1, 128]], small=True), W=["jrow"])
+    op("g", iota(T.n16[:], [[16, 32]], small=True), W=["n16"])
+    op("g", iota(T.ui[:], [[1, 2], [16, 8]]), W=["ui"])
+    op("g", iota(k4, [[1, 4]], small=True), W=["k4"])
+    op("v", lambda: V.memset(T.r13[:], 1.0), W=["ones"])
+    for b in (0, 1):
+        op("g", lambda: g.affine_select(T.et[:, 512 * b:512 * b + 512], T.r13[:, 0:512], [[4, 128], [1, 4]], A.is_equal, 0.0, -b, -4),
+           R=["ones"], W=["et%d" % b])
+    op("g", iota(T.ri[:, 0:50], [[20, 25], [0, 2]], 19), W=["ri0"])
+    op("g", iota(T.ri[:, 50:76], [[16, 26]], 15), W=["ri1"])
+    op("g", iota(T.qrow[:], [[0, 25], [1, 16]], small=True), W=["qrow"])
+    op("v", lambda: V.memset(T.et[:, 1024:2048], 0.0), W=["et"])
+    fill(T.r20m[:], 512, 1.0, ["r20m"])
+    fill(T.r16[:], 832, 1.0, ["r16"])
+    fill(T.r20m[:, 0:512:20], 26, 0.0, ["r20m"])
+    fill(T.r16[:, 0:832:16], 52, 0.0, ["r16"])
+    fill(T.wv[:, SL - 1:SL * 208:SL], 208, 0.0, ["wz"])
+    op("s", act(T.r20a[:], T.r20m[:], ACT.Identity, scale=1e29, bias=-1e29), R=["r20m"], W=["r20a"])
+    op("v", cp(col(10), T.pi[:]), R=["pi"], W=["pf"])
+    op("v", ts(T.pb[:, 0:1], T.pi[:], 15, None, A.bitwise_and), R=["pi"], W=["pb0"])
+    op("v", ts(T.pb[:, 1:2], T.pi[:], 16, None, A.bitwise_and), R=["pi"], W=["pb1"])
+    op("v", ts(T.pb[:, 2:3], T.pi[:], 2, 3, A.logical_shift_right, A.bitwise_and), R=["pi"], W=["pb2"])
+    op("v", ts(T.pb[:, 3:4], T.pi[:], 3, None, A.bitwise_and), R=["pi"], W=["pb3"])
+    op("v", ts(T.pb[:, 4:5], T.pi[:], 4, 1, A.logical_shift_right, A.bitwise_and), R=["pi"], W=["pb4"])
+    op("v", ts(T.pb[:, 5:6], T.pi[:], 1, None, A.bitwise_and), R=["pi"], W=["pb5"])
+    for b in (2, 3):
+        op("v", ts(T.et[:, 512 * b + b:512 * b + 512:4], T.jrow[:], col(10), None, A.is_equal), R=["jrow", "pf", "et"], W=["et%d" % b])
+    op("v", cp(T.pc[:, 0:6], T.pb[:, 0:6]), R=["pb%d" % i for i in range(6)], W=["pc"])
+    op("v", cp(T.uo[:], T.ui[:]), R=["ui"], W=["uo"])
+    q, h16, iq, jq, odd, par = [col(i) for i in range(6)]
+    op("v", ts(T.nn[:], T.n16[:], q, None, A.add), R=["n16", "pc"], W=["nn"])
+    op("v", ts(T.km[:, 8:12], k4, jq, None, A.is_equal), R=["k4", "pc"], W=["mj"])
+    op("v", ts(T.ca[:, 0:32], T.nn[:], 0.05, -0.475, A.mult, A.add), R=["nn"], W=["ca0"])
+    op("v", ts(T.ca[:, 32:64], T.nn[:], 0.01, -0.495, A.mult, A.add), R=["nn"], W=["ca1"])
+    op("v", ts(T.km[:, 4:8], k4, iq, None, A.is_equal), R=["k4", "pc"], W=["mi"])
+    op("v", cp(T.cb[:, 0:64], T.ca[:, 0:64]), R=["ca0", "ca1"], W=["cb0"])
+    op("v", quant(T.uq[:], T.usc[:], T.uin[:]), R=["uin"], W=["uq"])
+    op("v", cp(T.urq[:].bitcast(dt.uint32), T.uq[:].bitcast(dt.uint32).indirect(T.uo[:])), R=["uq", "uo"], W=["urq"])
+    op("s", act(T.ursc[:], T.usc[:].indirect(T.uo[:]), ACT.Copy), R=["uq", "uo"], W=["ursc"])
+    fill(T.wo[:, SL - 1:SL * 16:SL], 16, 0.0, ["woz0"])
+    fill(T.wo[:, SL * 416 + SL - 1:SL * 432:SL], 16, 0.0, ["woz1"])
+    fill(T.ew[:, 0:16], 16, 0.0, ["ewz"])
+    fill(T.acc[:], 32, 0.0, ["acc%d" % t for t in range(NP)])
+    fill(T.acc2[:], 32, 0.0, ["acb%d" % t for t in range(NP)])
+    fill(p1, 32, 0.0, ["p1"])
+    op("s", act(T.cl[:, 64:96], T.nn[:], ACT.Identity, bias=K - RB), R=["nn"], W=["cl2"])
+    f20, f100, f5 = T.cb[:, 0:32], T.cb[:, 32:64], T.cb[:, 64:96]
+    c = [T.cc[:, 32 * i:32 * i + 32] for i in range(8)]
+    op("v", ts(c[0], f20, -20.0, None, A.mult), R=["cb0"], W=["c0"])
+    op("v", ts(c[1], f100, -100.0, None, A.mult), R=["cb0"], W=["c1"])
+    op("v", ts(c[2], f100, 20.0, None, A.mult), R=["cb0"], W=["c2"])
+    op("v", tt(c[3], c[0], T.nn[:], A.add), R=["c0", "nn"], W=["c3"])
+    op("v", tt(T.cl[:, 32:64], c[1], T.nn[:], A.add), R=["c1", "nn"], W=["cl1"])
+    op("v", ts(col(6), odd, par, 432.0, A.not_equal, A.mult), R=["pc"], W=["pc6"])
+    op("v", ts(col(7), odd, par, 176.0, A.not_equal, A.mult), R=["pc"], W=["pc7"])
+    op("v", ts(col(9), jq, 5.0 * L, None, A.mult), R=["pc"], W=["pc9"])
+    op("v", ts(T.lh[:, 32:34], T.nn[:, 0:2], 16.0, col(6), A.mult, A.add), R=["nn", "pc6"], W=["lh2"])
+    op("v", quant(T.xq0[:], T.xs0[:], T.xin[:]), R=["xin0", "xin1"], W=["xq0"])
+    op("v", tt(T.cl[:, 0:32], c[2], c[3], A.add), R=["c2", "c3"], W=["cl0"])
+    op("v", cp(T.co[:, 32:64], T.cl[:, 32:64]), R=["cl1"], W=["coB"])
+
+    def more_constants():
+        op("v", quant(T.eq[:], T.esc[:], T.et[:]), R=["et0", "et1", "et2", "et3"], W=["eq"])
+        op("g", iota(T.vcb[:, 0:NP], [[1023 * L, 5], [L, 5]], C, small=True), W=["vcb"])
+        op("v", ts(T.co[:, 0:32], T.cl[:, 0:32], 99.0, None, A.min), R=["cl0"], W=["coA"])
+        op("v", ts(T.ca[:, 64:96], c[3], 0.2, -0.4, A.mult, A.add), R=["c3"], W=["ca2"])
+
+    def later_constants():
+        op("v", ts(c[4], f20, 160.0, h16, A.mult, A.add), R=["cb0", "pc"], W=["c4"])
+        op("v", cp(f5, T.ca[:, 64:96]), R=["ca2"], W=["cb2"])
+        op("v", ts(c[5], f100, -796.0, None, A.mult), R=["cb0"], W=["c5"])
+        op("v", ts(c[6], c[3], 32.0, None, A.mult), R=["c3"], W=["c6"])
+        op("v", ts(c[7], f5, -159.0, None, A.mult), R=["cb2"], W=["c7"])
+        op("v", tt(c[0], c[4], c[5], A.add), R=["c4", "c5"], W=["c0"])
+        op("v", tt(c[1], c[6], c[7], A.add), R=["c6", "c7"], W=["c1"])
+        op("v", cp(T.ro[:], T.ri[:]), R=["ri0", "ri1"], W=["ro"])
+        op("v", tt(T.cl[:, 96:128], c[0], c[1], A.add), R=["c0", "c1"], W=["cl3"])
+        op("v", ts(T.co[:, 64:96], f20, 32.0, 799.0, A.mult, A.min), R=["cb0"], W=["coR"])
+        op("v", cp(T.co[:, 96:122], T.cl[:, 96:122]), R=["cl3"], W=["coN"])
+        op("v", ts(T.dmask[:], T.qrow[:], q, None, A.is_equal), R=["qrow", "pc"], W=["dmask"])
+        op("v", ts(T.smask[:], T.qrow[:], q, None, A.is_gt), R=["qrow", "pc"], W=["smask"])
+        op("v", ts(T.pb[:, 6:7], T.pi[:], 4, None, A.logical_shift_right), R=["pi"], W=["gi"])
+        op("v", ts(T.lh[:, 36:38], T.nn[:, 0:2], 16.0, col(7), A.mult, A.add), R=["nn", "pc7"], W=["lh3"])
+        op("v", ts(T.cl[:, 128:160], f20, 5.0, None, A.mult), R=["cb0"], W=["m0"])
+        op("v", ts(T.cl[:, 160:192], f100, 75.0, None, A.mult), R=["cb0"], W=["m1"])
+        op("v", ts(T.cl[:, 192:224], f5, 20.0, None, A.mult), R=["cb2"], W=["m2"])
+        op("v", ts(col(8), iq, 5115.0 * L, col(9), A.mult, A.add), R=["pc", "pc9"], W=["pc8"])
+        op("v", tt(T.cl[:, 128:160], T.cl[:, 128:160], T.cl[:, 160:192], A.add), R=["m0", "m1"], W=["m0"])
+        op("v", tt(T.cl[:, 192:224], T.cl[:, 192:224], c[3], A.add), R=["m2", "c3"], W=["m2"])
+        op("v", ts(T.so[:, 0:2], T.lh[:, 32:34], 15.0, 831.0, A.add, A.min), R=["lh2"], W=["so"])
+        op("v", tt(T.cl[:, 224:256], T.cl[:, 128:160], T.cl[:, 192:224], A.add), R=["m0", "m2"], W=["m3"])
+        op("v", ts(T.so[:, 2:4], T.lh[:, 36:38], 351.0, None, A.min), R=["lh3"], W=["eo"])
+        op("v", cp(T.co[:, 128:154], T.cl[:, 224:250]), R=["m3"], W=["coM"])
+
+    listA, listB, listR, listN, listM = T.co[:, 0:32], T.co[:, 32:64], T.co[:, 64:96], T.co[:, 96:121], T.co[:, 128:153]
+
+    def win(b, n):
+        return T.w32[:, WW * b + C + K - n:WW * b + C + K]
+
+    def plane(b):
+        op("s", act(win(b, C), bank(b, C), ACT.Identity, scale=32.0), W=["w%d" % b], P=["b%d" % b])
+
+    def unpack(k, codes, scales, key):
+        for b in range(4):
+            op("t", mm(k + b, C, T.eq[:, 128 * b:128 * b + 128], T.esc[:, 128 * b:128 * b + 128], codes, scales), R=["eq", key], W=["b%d" % (k + b)])
+
+    for r in range(ROUNDS):
+        dst = partners[r]
+        wide = topo.mask(core, dst)
+        xq, xs, X = T["xq%d" % r], T["xs%d" % r], "xq%d" % r
+        out, land = T["out%d" % r], T["land%d" % r]
+        tq, tsc, lq, lsc = T["tq%d" % r], T["ts%d" % r], T["lq%d" % r], T["ls%d" % r]
+
+        for h in (1, 0):
+            op("t", mm(4 + h, 200, T.urq[:, 128:256], T.ursc[:, 128:256], xq[:, 200 * h:200 * h + 200], xs[:, 200 * h:200 * h + 200]),
+               R=["urq", "ursc", X], W=["b%d" % (4 + h)])
+        op("t", mm(6, C, T.urq[:, 0:128], T.ursc[:, 0:128], xq[:], xs[:]), R=["urq", "ursc", X], W=["b6"])
+        for k in range(2):
+            op("v", ts(T.sel1[:, 100 * k:100 * k + 100], bank(4, 100, 100 * k), T.km[:, 8 + k:9 + k], None, A.mult), R=["mj"], W=["sel1%d" % k], P=["b4"])
+            op("s", act(T.sel1[:, 200 + 100 * k:300 + 100 * k], bank(5, 100, 100 * k), ACT.Identity, scale=T.km[:, 10 + k:11 + k]),
+               R=["mj"], W=["sel1%d" % (2 + k)], P=["b5"])
+        for k in range(2):
+            op("v", tt(T.sel1h[:, 100 * k:100 * k + 100], T.sel1[:, 100 * k:100 * k + 100], T.sel1[:, 200 + 100 * k:300 + 100 * k], A.add),
+               R=["sel1%d" % k, "sel1%d" % (2 + k)], W=["sel1h%d" % k])
+        op("v", tt(out[:], T.sel1h[:, 0:100], T.sel1h[:, 100:200], A.add), R=["sel1h0", "sel1h1"], W=["out%d" % r])
+        send(dst, land[:], out[:], "arrs%d" % r, common, ["out%d" % r])
+        writer["land%d" % r] = ("arrs%d" % r, engines_of(common))
+        count["arrs%d" % r] = engines_of(common)
+
+        for k in range(4):
+            op("s", act(T.sel0[:, 100 * k:100 * k + 100], bank(6, 100, 100 * k), ACT.Identity, scale=T.km[:, 4 + k:5 + k]),
+               R=["mi"], W=["sel0%d" % k], P=["b6"])
+        if r == 0:
+            more_constants()
+        unpack(0, xq[:], xs[:], X)
+        if r > 0:
+            op("v", cp(T.tt[:, 2:4 * C:4], bank(2, C)), W=["tt2"], P=["b2"])
+        op("v", tt(T.sel0h[:], T.sel0[:, 0:200], T.sel0[:, 200:400], A.add), R=["sel00", "sel01", "sel02", "sel03"], W=["sel0h"])
+        op("s", act(T.tt[:, 0:4 * C:4], bank(0, C), ACT.Copy), W=["tt0"], P=["b0"])
+        op("v", tt(T.a0[:], T.sel0h[:, 0:100], T.sel0h[:, 100:200], A.add), R=["sel0h"], W=["a0"])
+        op("s", act(T.aexp[:], T.a0[:].indirect(listA), ACT.Copy), R=["a0", "coA"], W=["aexp"])
+        if r == 0:
+            later_constants()
+            op("s", act(T.tt[:, 2:4 * C:4], bank(2, C), ACT.Copy), W=["tt2"], P=["b2"])
+        op("v", cp(T.tt[:, 3:4 * C:4], bank(3, C)), W=["tt3"], P=["b3"])
+        op("s", act(T.tt[:, 1:4 * C:4], bank(1, C), ACT.Copy), W=["tt1"], P=["b1"])
+        op("v", quant(tq[:], tsc[:], T.tt[:]), R=["tt0", "tt1", "tt2", "tt3"], W=["tq%d" % r])
+        send(dst, u8(lq[:]), u8(tq[:]), "arrc%d" % r, wide, ["tq%d" % r])
+        send(dst, lsc[:], tsc[:], "arrc%d" % r, wide, ["tq%d" % r])
+        writer["lq%d" % r] = ("arrc%d" % r, 2 * engines_of(wide))
+        count["arrc%d" % r] = 2 * engines_of(wide)
+        if r == 0:
+            for u in range(SL, NP):
+                fill(T.wv[:, SL * 16 * u + u - SL:SL * 16 * (u + 1):SL], 16, 0.0, ["wz%d" % u])
+            op("s", act(T.r13[:, 0:SL * CW:SL], T.r16[:, 0:CW], ACT.Identity, scale=0.0), R=["r16"], W=["r13", "ones"])
+            dma("y", u8(T.wq[:]), T.wc[:], R=["land0"], W=["wq"])
+            dma("y", T.wsc[:], T.ws[:], W=["wsc"])
+            dma("y", T.vin[:], T.v[:], W=["vin"])
+        else:
+            plane(0)
+            plane(2)
+        if r == 1:
+            op("v", quant(T.vq[:], T.vsc[:], T.vin[:]), R=["vin"], W=["vq"])
+
+        op("v", tt(T.sums[:], land[:].indirect(listB), T.aexp[:], A.add), R=["land%d" % r, "coB", "aexp"], W=["sums"])
+        op("v", scan(T.rmax[:], T.r20a[:], T.sums[:], A.add, A.max), R=["r20a", "sums"], W=["rmax"])
+        op("v", cp(T.brep[:, 0:256], T.rmax[:].indirect(T.ro[:, 0:16])), R=["rmax", "ro"], W=["brep0"])
+        op("s", act(T.brep[:, 256:512], T.rmax[:].indirect(T.ro[:, 16:32]), ACT.Copy), R=["rmax", "ro"], W=["brep1"])
+        op("s", act(T.brep[:, 512:800], T.rmax[:].indirect(T.ro[:, 32:50]), ACT.Copy), R=["rmax", "ro"], W=["brep2"])
+        for k, (a, z) in enumerate(((0, 256), (256, 512), (512, 800))):
+            op("v", turn(T.btr[:, a:z], T.brep[:, a:z]), R=["brep%d" % k], W=["btr%d" % k])
+        btr = ["btr0", "btr1", "btr2", "coN"]
+        plane(3)
+        op("s", act(T.row[:], T.btr[:].indirect(listN), ACT.Copy), R=btr, W=["row"])
+        op("v", tt(T.rowd[:], T.btr[:].indirect(listN), T.dmask[:], A.mult), R=btr + ["dmask"], W=["rowd"])
+        plane(1)
+        op("v", scan(T.piv[:], T.r16[:, 0:C], T.rowd[:], A.mult, A.add), R=["r16", "rowd"], W=["piv"])
+
+        def pivot(t):
+            return T.piv[:, 16 * t + 15:16 * t + 16]
+
+        def slots(t, a, z):
+            return T.wv[:, SL * a + t % SL:SL * z:SL]
+
+        def parts(t):
+            a, z = 16 * (t + 1), 16 * (t + 1 + NB)
+            return ([(a, min(z, C), A.is_gt, "a")] if a < C else []) + ([(0, z - C, A.is_ge, "b")] if z > C else [])
+
+        def sign(t):
+            op("s", act(T.sg[:, 192 * t:192 * t + 192], T.row[:, 16 * t + 16:16 * t + 208], ACT.Sign, bias=pivot(t), scale=-1.0), R=["row", "piv"], W=["sg%d" % t])
+
+        def keep(t):
+            op("s", act(slots(t, 16 * t + 16, 16 * t + 208), T.sg[:, 192 * t:192 * t + 192], ACT.Relu, scale=-1.0, accum_out=T.acc[:, t:t + 1]),
+               R=["sg%d" % t], W=["wa%d" % t, "acc%d" % t])
+
+        def compare(t):
+            for a, z, o, s in parts(t):
+                op("v", ts(slots(t, a, z), T.row[:, a:z], pivot(t), None, o), R=["row", "piv"], W=["w%s%d" % (s, t)])
+
+        def tally(t, i):
+            a, z, o, s = parts(t)[i]
+            j = 192 * t + (0 if i == 0 else 192 - z)
+            op("s", act(T.junk[:, j:j + z - a], slots(t, a, z), ACT.Copy, accum_out=(T.acc2 if i else T.acc)[:, t:t + 1]),
+               R=["w%s%d" % (s, t)], W=["junk%d%d" % (i, t), ("acb%d" if i else "acc%d") % t])
+
+        def columns(k):
+            a, z = CW * k, CW * k + CW
+            keys = ["w%s%d" % (p[3], t) for t in range(NP) for p in parts(t) if p[0] < z and p[1] > a]
+            op("v", scan(T.wo[:, SL * (16 + a):SL * (16 + z)], T.r13[:], T.wv[:, SL * a:SL * z], A.mult, A.add),
+               R=keys + ["r13", "wz"] + ["wz%d" % u for u in range(SL, NP)], W=["wo%d" % k])
+
+        sign(0)
+        op("v", tt(T.lt[:], T.brep[:].indirect(listR), T.rmax[:], A.is_gt), R=["rmax", "brep0", "brep1", "brep2", "coR"], W=["lt"])
+        compare(NP - 1)
+        op("v", scan(T.mid[:], T.r20m[:], T.lt[:], A.mult, A.add), R=["r20m", "lt"], W=["mid"])
+        compare(NP - 2)
+        op("v", ts(T.vblk[:, 32:32 + NP], T.mid[:, 19:500:20], 1024.0, col(8), A.mult, A.add), R=["mid", "pc8"], W=["vb0"])
+        compare(NP - 3)
+        op("v", tt(T.vblk[:, 0:NP], T.vblk[:, 32:32 + NP], T.vcb[:, 0:NP], A.add), R=["vb0", "vcb"], W=["vblk"])
+        dma("y", T.tbl[:], T.vblk[:, 0:NP], R=["vblk"], W=["tbl"])
+        order("g", ["tbl", "gi"], ["vrep"], ())
+        g.indirect_dma_start(T.vrep[:], None, T.tbl[:], IndirectOffsetOnAxis(ap=T.pb[:, 6:7], axis=0), bounds_check=7).then_inc(T.sem.rows, 16)
+        count["rows"] = count.get("rows", 0) + 16
+        done(("rows", count["rows"]), ["tbl", "gi"], ["vrep"], ())
+        for t in range(NP - 4, NS - 1, -1):
+            compare(t)
+        for t in range(NS):
+            if t + 1 < NS:
+                sign(t + 1)
+            keep(t)
+        op("v", tt(T.dif[:], T.piv[:].indirect(T.ro[:, 50:75]), T.row[:], A.subtract), R=["piv", "ro", "row"], W=["dif"])
+        unpack(4, lq[:], lsc[:], "lq%d" % r)
+        for t in range(NS, NP):
+            if len(parts(t)) > 1:
+                tally(t, 1)
+        for t in range(NS, NP):
+            tally(t, 0)
+        op("s", act(T.vrow[:], T.vrep[:].indirect(listM), ACT.Copy), R=["vrep", "coM"], W=["vrow"])
+        columns(0)
+        op("v", ts(T.ged[:], T.dif[:], 0.0, None, A.is_le), R=["dif"], W=["ged"])
+        op("v", ts(T.eqd[:], T.dif[:], 0.0, None, A.is_equal), R=["dif"], W=["eqd"])
+        op("v", scan(T.ges[:], T.r16[:, 0:C], T.ged[:], A.mult, A.add), R=["ged", "r16"], W=["ges"])
+        op("v", scan(T.eqs[:], T.eqd[:], T.smask[:], A.add, A.mult), R=["eqd", "smask"], W=["eqs"])
+        columns(1)
+        op("v", tt(T.pp[:, 0:NP], T.ges[:, 15:C:16], T.eqs[:, 15:C:16], A.subtract), R=["ges", "eqs"], W=["p1"])
+        for k in range(2, C // CW):
+            columns(k)
+        wo = ["wo%d" % k for k in range(C // CW)] + ["woz0", "woz1"]
+        op("v", tt(p2, p1, T.acc2[:], A.add), R=["p1"] + ["acb%d" % t for t in range(NP)], W=["p2"])
+        op("v", turn(T.ctr[:, 0:416], T.wo[:, SL * 16 + SL - 1:SL * 432:SL]), R=wo, W=["ctr0"])
+        op("v", turn(T.ctr[:, 416:832], T.wo[:, SL - 1:SL * 416:SL]), R=wo, W=["ctr1"])
+        op("v", scan(T.cseg[:], T.r16[:], T.ctr[:], A.mult, A.add), R=["r16", "ctr0", "ctr1"], W=["cseg"])
+        op("v", tt(p3, p2, T.acc[:], A.add), R=["p2"] + ["acc%d" % t for t in range(NP)], W=["p3"])
+        op("v", tt(T.nrk[:], T.cseg[:].indirect(T.so[:, 0:2]), p3, A.subtract), R=["cseg", "so", "p3"], W=["nrk"])
+        op("v", ts(T.rko[:, 0:NP], T.nrk[:, 0:NP], -1.0, RB + 16.0, A.mult, A.add), R=["nrk"], W=["rko"])
+        op("s", act(T.xa[:, 0:NP], T.nrk[:, 0:NP], ACT.Relu, scale=-1000.0, bias=1000.0 * (RB - K + 1)), R=["nrk"], W=["xa0"])
+        if r == 0:
+            plane(0)
+            plane(2)
+        for b in range(4):
+            op("s", act(T.tb[:, C * b:C * b + C], bank(4 + b, C), ACT.Identity, scale=0.5), W=["tb%d" % b], P=["b%d" % (4 + b)])
+        op("v", cp(T.ew[:].indirect(T.rko[:, 0:NP]), T.vrow[:]), R=["vrow", "rko", "ewz"], W=["ew"])
+        op("v", turn(T.etr[:, 0:K], T.ew[:, 16:K + 16]), R=["ew"], W=["etr0"])
+        op("v", turn(T.etr[:, K:352], T.ew[:, 0:192]), R=["ew"], W=["etr1"])
+        op("v", cp(T.li[:, 0:16], T.etr[:].indirect(T.so[:, 2:3])), R=["etr0", "etr1", "eo"], W=["li"])
+        la, ld = T.lj[:, 0:10], T.lb[:, 0:10]
+        op("v", ts(la, T.li[:, 0:10], 10, None, A.logical_shift_right), R=["li"], W=["lj0"])
+        op("v", ts(ld, T.li[:, 0:10], 1023, None, A.bitwise_and), R=["li"], W=["lj1"])
+        op("v", cp(T.la[:, 0:10], la), R=["lj0"], W=["la"])
+        op("v", tt(T.lj[:, 10:20], la, ld, A.add), R=["lj0", "lj1"], W=["lb"])
+        op("v", ts(T.lo[:, 0:10], T.lj[:, 10:20], -float(C), None, A.add), R=["lb"], W=["lo"])
+        op("v", ts(T.lf[:, 0:20], T.lj[:, 0:20], 0.05, -0.475, A.mult, A.add), R=["lj0", "lb"], W=["lf0"])
+        for b in range(4):
+            op("s", act(T.ah[:, K * b:K * b + K], win(b, C).indirect(T.la[:, 0:10]), ACT.Identity, scale=2.0 ** -6), R=["w%d" % b, "la"], W=["ah%d" % b])
+        op("v", cp(T.lg[:, 0:20], T.lf[:, 0:20]), R=["lf0"], W=["lg"])
+
+        def zpart(b):
+            op("v", tt(T.zt[:, b:4 * K:4], T.tb[:, C * b:C * b + C].indirect(T.lo[:, 0:10]), T.ah[:, K * b:K * b + K], A.add),
+               R=["tb%d" % b, "lo", "ah%d" % b], W=["zt%d" % b])
+        zpart(0)
+        op("v", ts(T.lh[:, 0:10], T.lg[:, 0:10], 20.0, -20.0, A.mult, A.add), R=["lg"], W=["lh0"])
+        zpart(1)
+        op("v", tt(T.lh[:, 16:26], T.lh[:, 0:10], T.lg[:, 10:20], A.add), R=["lh0", "lg"], W=["lh1"])
+        op("v", cp(T.le[:, 0:10], T.lh[:, 16:26]), R=["lh1"], W=["le"])
+        zpart(2)
+        zpart(3)
+        for b in range(4):
+            op("s", act(T.te[:, K * b:K * b + K], win(b, C).indirect(T.le[:, 0:10]), ACT.Copy), R=["w%d" % b, "le"], W=["te%d" % b])
+        op("v", quant(T.zq[:], T.zsc[:], T.zt[:]), R=["zt0", "zt1", "zt2", "zt3"], W=["zq"])
+        for b in range(4):
+            op("t", mm(4 + b, K, T.wq[:, 128 * b:128 * b + 128], T.wsc[:, 128 * b:128 * b + 128], T.zq[:], T.zsc[:]),
+               R=["wq", "wsc", "zq"], W=["b%d" % (4 + b)])
+        xa = [T.xa[:, 32 * i:32 * i + NP] for i in range(3)]
+        op("v", tt(xa[1], xa[0], T.nrk[:, 0:NP], A.subtract), R=["nrk", "xa0"], W=["xa1"])
+        op("v", tt(xa[2], xa[1], T.cl[:, 64:64 + NP], A.min), R=["xa1", "cl2"], W=["xa2"])
+        op("v", ts(T.xo[:, 0:NP], xa[2], RB, None, A.add), R=["xa2"], W=["xo"])
+        for b in range(4):
+            op("v", tt(T.w32[:, WW * b:WW * b + K], bank(4 + b, K), T.te[:, K * b:K * b + K], A.add),
+               R=["te%d" % b], W=["n%d" % b], P=["b%d" % (4 + b)])
+        for b, a, z, e in ((0, 0, NP, "s"), (3, 0, NP, "v"), (1, 0, NP, "s"), (2, 12, NP, "v"), (2, 0, 12, "s")):
+            o, w = T.xt[:, 64 * a + b:64 * z:4], win(b, C + K).indirect(T.xo[:, a:z])
+            call = act(o, w, ACT.Identity, scale=2.0 ** -5) if e == "s" else ts(o, w, 2.0 ** -5, None, A.mult)
+            op(e, call, R=["w%d" % b, "n%d" % b, "xo"], W=["xt%d%s" % (b, e)])
+        op("v", quant(T["xq%d" % (r + 1)][:], T["xs%d" % (r + 1)][:], T.xt[:]), R=["xt0s", "xt1s", "xt2s", "xt2v", "xt3v"], W=["xq%d" % (r + 1)])
+
+    xq, xs, X = T["xq%d" % ROUNDS], T["xs%d" % ROUNDS], "xq%d" % ROUNDS
+    for h in (1, 0):
+        op("t", mm(h, 200, T.vq[:], T.vsc[:], xq[:, 200 * h:200 * h + 200], xs[:, 200 * h:200 * h + 200]), R=["vq", X], W=["b%d" % h])
+    dma("y", T.oc[:], u8(xq[:]), R=[X])
+    op("v", cp(T.yo[:, 0:200], bank(0, 200)), W=["yo0"], P=["b0"])
+    op("s", act(T.yo[:, 200:400], bank(1, 200), ACT.Copy), W=["yo1"], P=["b1"])
+    dma("y", T.osc[0:4, :], xs[0:4, :], R=[X])
+    dma("y", T.y[:, 0:200], T.yo[:, 0:200], R=["yo0"])
+    dma("s", T.y[:, 200:400], T.yo[:, 200:400], R=["yo1"])
+    dma("y", T.osc[4:8, :], xs[32:36, :], R=[X])
+    dma("s", T.osc[8:12, :], xs[64:68, :], R=[X])
+    dma("s", T.osc[12:16, :], xs[96:100, :], R=[X])
+    need("g", list(count.items()))

@@ -1,34 +1,37 @@
-from concourse.bass import IndirectOffsetOnAxis
 from concourse.mybir import dt, AluOpType, ActivationFunctionType
 
 C, L, K, ROUNDS = 400, 20, 160, 3
 MASKS = [1, 2, 3]
 NP = 25
 NB = 12
-SL = 13
-NS = 11
-CW = 80
-RB = 16.0 * NB - 1
+V0, V1 = 13, 24
+EARLY = 0
+SL = 7
+PAD = 160
+GROUPS = [(16, 25), (8, 16), (0, 8)]
 WW = 576
+BIG = 2.0 ** 90
+UP = 136.0
 
-F32, BF, I32, U16, X4, U8 = "float32", "bfloat16", "int32", "uint16", "float8_e4m3fn_x4", "uint8"
-SCRATCH = {"ps": ("psum", [128, 4096], F32), "tbl": ("dram", [8, C], F32)}
+F32, BF, F16, I32, U16, X4, U8 = "float32", "bfloat16", "float16", "int32", "uint16", "float8_e4m3fn_x4", "uint8"
+SCRATCH = {"ps": ("psum", [128, 4096], F32)}
 for _d, _l in (
-    (BF, dict(xin=4 * C, uin=512, vin=512, et=2048, qrow=C, dmask=C, smask=C, r20m=512, r16=832, r13=SL * CW, lt=512, mid=512,
-              dif=C, eqd=C, eqs=C, ged=C, ges=C, wv=SL * C, wo=SL * 432, sg=SL * 192, junk=NP * 192, ctr=832, cseg=832,
+    (BF, dict(xin=4 * C, uin=512, vin=512, et=516, ones=520, quo=128, qrow=C, pen=C, rst=C, r20m=520, r16=416, r4=C, mjt=200, lt=512, mid=512,
+              wv=2 * SL * (PAD + C), dsum=C, junk=176 * 16, sg=4 * 192, cs=432, ctr=832, cseg=960,
               tt=4 * C, w32=4 * WW, tb=4 * C, ah=4 * K, te=4 * K, zt=4 * K, xt=4 * C)),
-    (F32, dict(pc=12, km=12, jrow=128, n16=32, nn=32, ca=96, cc=256, cl=256, r20a=512, sel1=C, sel1h=200, sel0=C, sel0h=200,
-               a0=100, aexp=512, sums=512, rmax=512, brep=800, btr=800, row=C, rowd=C, piv=C, acc=32, acc2=32, pp=96, nrk=32,
-               vblk=64, vcb=32, vrep=C, vrow=C, ew=C + 16, etr=352, lf=32, lh=48, xa=96, yo=C,
+    (F16, dict(cum=SL * (C + 8))),
+    (F32, dict(pc=20, km=12, n16=32, nn=32, left=32, terms=608, tsum=840, r20a=512, sel1=C, sel1h=200, sel0=C, a0=C + 48,
+               aexp=512, sums=512, rmax=528, best=32, brep=432, btr=800, row=C, rowz=C, piv=C, pq=128, pp=128, nrk=32, seq=32,
+               vblk=64, vcb=96, vrep=C, vrow=C, ew=C + 16, etr=2 * K, xa=96, yo=C,
                out0=100, out1=100, out2=100, land0=100, land1=100, land2=100)),
-    (I32, dict(pi=1, pb=8, ui=16, cb=96, ri=76, li=16, lj=32, lg=32, lb=16)),
-    (U16, dict(uo=16, co=160, ro=76, so=4, rko=32, la=16, lo=16, le=16, xo=32)),
+    (I32, dict(pi=1, pb=8, ui=16)),
+    (U16, dict(uo=16, co=210, rko=32, lst=32, xo=32)),
     (X4, dict(wq=512, uq=128, urq=256, vq=128, eq=512, zq=K, xq0=C, xq1=C, xq2=C, xq3=C, tq0=C, tq1=C, tq2=C, lq0=C, lq1=C, lq2=C)),
     (U8, dict(wsc=512, usc=128, ursc=256, vsc=128, esc=512, zsc=K, xs0=C, xs1=C, xs2=C, xs3=C, ts0=C, ts1=C, ts2=C, ls0=C, ls1=C, ls2=C)),
 ):
     for _n, _w in _l.items():
         SCRATCH[_n] = ("sbuf", [128, _w], _d)
-SEMAPHORES = (["cv", "cs", "ct", "cg", "sent", "rows"] + ["d%d" % _i for _i in range(20)]
+SEMAPHORES = (["cv", "cs", "ct", "cg", "sent"] + ["d%d" % _i for _i in range(24)]
               + ["arrs%d" % _r for _r in range(ROUNDS)] + ["arrc%d" % _r for _r in range(ROUNDS)])
 
 A = AluOpType
@@ -44,8 +47,35 @@ def rank_program(g, core, T, topo):
     own = {"v": "cv", "s": "cs", "t": "ct", "g": "cg"}
     count = {}
     waited = {e: {} for e in queue}
-    writer, readers = {}, {}
+    touched = {}
     ndma = [0]
+
+    def bits(a, z, step=1):
+        n = (z - a + step - 1) // step
+        return ((1 << (n * step)) - 1) // ((1 << step) - 1) << a
+
+    def at(name, a=0, z=None, step=1):
+        if z is None:
+            z = SCRATCH[name][1][1]
+        return (T[name][:, a:z:step], [(name, bits(a, z, step))])
+
+    def by(win, off):
+        return (win[0].indirect(off[0]), win[1] + off[1])
+
+    def words(view):
+        return (view[0].bitcast(dt.uint32), view[1])
+
+    def u8(view):
+        return (view[0].bitcast(dt.uint8), view[1])
+
+    def bank(k, n, a=0):
+        return (T.ps[:, 512 * k + a:512 * k + a + n], [("bank%d" % k, 1)])
+
+    def hbm(ap):
+        return (ap, [])
+
+    def ap(x):
+        return x[0] if isinstance(x, tuple) else x
 
     def need(e, deps):
         top = {}
@@ -56,414 +86,491 @@ def rank_program(g, core, T, topo):
                 queue[e].wait_ge(T.sem[s], n)
                 waited[e][s] = n
 
-    def order(e, R, W, P):
-        deps = [writer[k] for k in list(R) + list(W) + list(P) if k in writer]
-        for k in W:
-            deps += readers.get(k, [])
-        for k in P:
-            deps += [d for d in readers.get(k, []) if d[0] != own.get(e)]
+    def order(e, R, W):
+        deps = []
+        for name, m in R:
+            deps += [x[1] for x in touched.get(name, []) if x[0] & m and (x[2] or (name[:4] == "bank" and x[1][0] != own.get(e)))]
+        for name, m in W:
+            deps += [x[1] for x in touched.get(name, []) if x[0] & m]
         need(e, deps)
 
-    def done(mark, R, W, P):
-        for k in list(R) + list(P):
-            readers.setdefault(k, []).append(mark)
-        for k in W:
-            writer[k] = mark
-            readers[k] = []
+    def done(mark, R, W):
+        for name, m in W:
+            touched[name] = [[x[0] & ~m, x[1], x[2]] for x in touched.get(name, []) if x[0] & ~m] + [[m, mark, True]]
+        for name, m in R:
+            touched.setdefault(name, []).append([m, mark, False])
 
-    def op(e, call, R=(), W=(), P=()):
-        order(e, R, W, P)
+    def regions(views):
+        return [r for v in views if isinstance(v, tuple) for r in v[1]]
+
+    def op(e, call, outs, ins):
+        R, W = regions(ins), regions(outs)
+        order(e, R, W)
         s = own[e]
         call().then_inc(T.sem[s], 1)
         count[s] = count.get(s, 0) + 1
-        done((s, count[s]), R, W, P)
+        done((s, count[s]), R, W)
 
-    def dma(e, out, in_, R=(), W=()):
-        order(e, R, W, ())
+    def dma(e, out, in_, after=()):
+        R, W = regions([in_] + list(after)), regions([out])
+        order(e, R, W)
         s = "d%d" % ndma[0]
         ndma[0] += 1
-        queue[e].dma_start(out, in_).then_inc(T.sem[s], 16)
+        queue[e].dma_start(out[0], in_[0]).then_inc(T.sem[s], 16)
         count[s] = 16
-        done((s, 16), R, W, ())
+        done((s, 16), R, W)
 
     def engines_of(m):
         return bin(m).count("1")
 
-    def send(dst, out, in_, sem, m, R):
-        order("g", R, (), ())
+    def send(dst, out, in_, sem, m):
+        order("g", in_[1], [])
         rid, pid = topo.addr(dst)[:2]
-        g.remote_dma(out, in_, T.sem[sem], T.sem.sent, pid, rid, m)
+        g.remote_dma(out[0], in_[0], T.sem[sem], T.sem.sent, pid, rid, m)
         count["sent"] = count.get("sent", 0) + engines_of(m)
+        count[sem] = count.get(sem, 0) + engines_of(m)
 
-    def bank(k, n, a=0):
-        return T.ps[:, 512 * k + a:512 * k + a + n]
-
-    def u8(view):
-        return view.bitcast(dt.uint8)
+    def arrives(sem, *views):
+        done((sem, count[sem]), [], regions(views))
 
     def ts(out, in0, s1, s2, o0, o1=None):
         if o1 is None:
-            return lambda: V.tensor_scalar(out, in0, s1, None, o0)
-        return lambda: V.tensor_scalar(out, in0, s1, s2, o0, o1)
+            op("v", lambda: V.tensor_scalar(out[0], in0[0], ap(s1), None, o0), [out], [in0, s1])
+        else:
+            op("v", lambda: V.tensor_scalar(out[0], in0[0], ap(s1), ap(s2), o0, o1), [out], [in0, s1, s2])
 
     def tt(out, in0, in1, o):
-        return lambda: V.tensor_tensor(out, in0, in1, o)
+        op("v", lambda: V.tensor_tensor(out[0], in0[0], in1[0], o), [out], [in0, in1])
 
     def cp(out, in_):
-        return lambda: V.tensor_copy(out, in_)
+        op("v", lambda: V.tensor_copy(out[0], in_[0]), [out], [in_])
 
-    def scan(out, d0, d1, o0, o1):
-        return lambda: V.tensor_tensor_scan(out, d0, d1, 0.0, o0, o1)
+    def scatter(win, off, in_):
+        op("v", lambda: V.tensor_copy(win[0].indirect(off[0]), in_[0]), [win], [off, in_])
+
+    def scan(out, d0, d1, o0, o1, first=0.0):
+        op("v", lambda: V.tensor_tensor_scan(out[0], d0[0], d1[0], ap(first), o0, o1), [out], [d0, d1, first])
 
     def turn(out, in_):
-        return lambda: V.transpose(out, in_)
+        op("v", lambda: V.transpose(out[0], in_[0]), [out], [in_])
 
     def quant(codes, plane, tile):
-        return lambda: V.quantize_mx(codes, plane, tile)
+        op("v", lambda: V.quantize_mx(codes[0], plane[0], tile[0]), [codes, plane], [tile])
 
-    def act(out, in_, f, **kw):
-        return lambda: S.activation(out, in_, f, **kw)
+    def mset(out, c):
+        op("v", lambda: V.memset(out[0], c), [out], [])
 
-    def fill(out, n, c, keys):
-        op("s", act(out, T.r13[:, 0:n], ACT.Identity, scale=0.0, bias=c), R=["ones"], W=keys)
+    def act(out, in_, f, total=None, **kw):
+        k = {n: ap(x) for n, x in kw.items()}
+        if total:
+            k["accum_out"] = total[0]
+        op("s", lambda: S.activation(out[0], in_[0], f, **k), [out, total], [in_] + list(kw.values()))
 
-    def iota(out, pattern, base=0, cm=0, small=False):
+    def line(out, in_, scale, bias=0.0):
+        act(out, in_, ACT.Identity, scale=scale, bias=bias)
+
+    def iota(out, pattern, base=0, cm=0, small=True):
         if small:
-            return lambda: g.iota(out, pattern, base, cm, allow_small_or_imprecise_dtypes=True)
-        return lambda: g.iota(out, pattern, base, cm)
+            op("g", lambda: g.iota(out[0], pattern, base, cm, allow_small_or_imprecise_dtypes=True), [out], [])
+        else:
+            op("g", lambda: g.iota(out[0], pattern, base, cm), [out], [])
+
+    def ones_where(name, pattern, compare, base=0, cm=0):
+        out, one = at(name), at("ones", 0, SCRATCH[name][1][1])
+        op("g", lambda: g.affine_select(out[0], one[0], pattern, compare, 0.0, base, cm), [out], [one])
 
     def mm(k, n, lq, ls, rq, rs):
-        return lambda: PE.matmul_mx(bank(k, n), lq, ls, rq, rs, True, True)
+        out = bank(k, n)
+        op("t", lambda: PE.matmul_mx(out[0], lq[0], ls[0], rq[0], rs[0], True, True), [out], [lq, ls, rq, rs])
 
-    def col(i):
-        return T.pc[:, i:i + 1]
+    def col(i, n=1):
+        return at("pc", i, i + n)
 
     partners = [T.cores[rank ^ s] for s in MASKS]
     common = topo.mask(core, partners[0])
     for d in partners:
         common &= topo.mask(core, d)
 
-    dma("s", T.uin[:], T.u[:], W=["uin"])
-    dma("y", T.xin[:, 0:800], T.x[:, 0:800], W=["xin0"])
-    dma("s", T.xin[:, 800:1600], T.x[:, 800:1600], W=["xin1"])
+    dma("s", at("uin"), hbm(T.u[:]))
+    dma("y", at("xin", 0, 800), hbm(T.x[:, 0:800]))
+    dma("s", at("xin", 800, 1600), hbm(T.x[:, 800:1600]))
 
-    k4, p1, p2, p3 = T.km[:, 0:4], T.pp[:, 0:32], T.pp[:, 32:64], T.pp[:, 64:96]
-    op("g", iota(T.pi[:], [[0, 1]], 0, 1), W=["pi"])
-    op("g", iota(T.jrow[:], [[1, 128]], small=True), W=["jrow"])
-    op("g", iota(T.n16[:], [[16, 32]], small=True), W=["n16"])
-    op("g", iota(T.ui[:], [[1, 2], [16, 8]]), W=["ui"])
-    op("g", iota(k4, [[1, 4]], small=True), W=["k4"])
-    op("v", lambda: V.memset(T.r13[:], 1.0), W=["ones"])
-    for b in (0, 1):
-        op("g", lambda: g.affine_select(T.et[:, 512 * b:512 * b + 512], T.r13[:, 0:512], [[4, 128], [1, 4]], A.is_equal, 0.0, -b, -4),
-           R=["ones"], W=["et%d" % b])
-    op("g", iota(T.ri[:, 0:50], [[20, 25], [0, 2]], 19), W=["ri0"])
-    op("g", iota(T.ri[:, 50:76], [[16, 26]], 15), W=["ri1"])
-    op("g", iota(T.qrow[:], [[0, 25], [1, 16]], small=True), W=["qrow"])
-    op("v", lambda: V.memset(T.et[:, 1024:2048], 0.0), W=["et"])
-    fill(T.r20m[:], 512, 1.0, ["r20m"])
-    fill(T.r16[:], 832, 1.0, ["r16"])
-    fill(T.r20m[:, 0:512:20], 26, 0.0, ["r20m"])
-    fill(T.r16[:, 0:832:16], 52, 0.0, ["r16"])
-    fill(T.wv[:, SL - 1:SL * 208:SL], 208, 0.0, ["wz"])
-    op("s", act(T.r20a[:], T.r20m[:], ACT.Identity, scale=1e29, bias=-1e29), R=["r20m"], W=["r20a"])
-    op("v", cp(col(10), T.pi[:]), R=["pi"], W=["pf"])
-    op("v", ts(T.pb[:, 0:1], T.pi[:], 15, None, A.bitwise_and), R=["pi"], W=["pb0"])
-    op("v", ts(T.pb[:, 1:2], T.pi[:], 16, None, A.bitwise_and), R=["pi"], W=["pb1"])
-    op("v", ts(T.pb[:, 2:3], T.pi[:], 2, 3, A.logical_shift_right, A.bitwise_and), R=["pi"], W=["pb2"])
-    op("v", ts(T.pb[:, 3:4], T.pi[:], 3, None, A.bitwise_and), R=["pi"], W=["pb3"])
-    op("v", ts(T.pb[:, 4:5], T.pi[:], 4, 1, A.logical_shift_right, A.bitwise_and), R=["pi"], W=["pb4"])
-    op("v", ts(T.pb[:, 5:6], T.pi[:], 1, None, A.bitwise_and), R=["pi"], W=["pb5"])
-    for b in (2, 3):
-        op("v", ts(T.et[:, 512 * b + b:512 * b + 512:4], T.jrow[:], col(10), None, A.is_equal), R=["jrow", "pf", "et"], W=["et%d" % b])
-    op("v", cp(T.pc[:, 0:6], T.pb[:, 0:6]), R=["pb%d" % i for i in range(6)], W=["pc"])
-    op("v", cp(T.uo[:], T.ui[:]), R=["ui"], W=["uo"])
-    q, h16, iq, jq, odd, par = [col(i) for i in range(6)]
-    op("v", ts(T.nn[:], T.n16[:], q, None, A.add), R=["n16", "pc"], W=["nn"])
-    op("v", ts(T.km[:, 8:12], k4, jq, None, A.is_equal), R=["k4", "pc"], W=["mj"])
-    op("v", ts(T.ca[:, 0:32], T.nn[:], 0.05, -0.475, A.mult, A.add), R=["nn"], W=["ca0"])
-    op("v", ts(T.ca[:, 32:64], T.nn[:], 0.01, -0.495, A.mult, A.add), R=["nn"], W=["ca1"])
-    op("v", ts(T.km[:, 4:8], k4, iq, None, A.is_equal), R=["k4", "pc"], W=["mi"])
-    op("v", cp(T.cb[:, 0:64], T.ca[:, 0:64]), R=["ca0", "ca1"], W=["cb0"])
-    op("v", quant(T.uq[:], T.usc[:], T.uin[:]), R=["uin"], W=["uq"])
-    op("v", cp(T.urq[:].bitcast(dt.uint32), T.uq[:].bitcast(dt.uint32).indirect(T.uo[:])), R=["uq", "uo"], W=["urq"])
-    op("s", act(T.ursc[:], T.usc[:].indirect(T.uo[:]), ACT.Copy), R=["uq", "uo"], W=["ursc"])
-    fill(T.wo[:, SL - 1:SL * 16:SL], 16, 0.0, ["woz0"])
-    fill(T.wo[:, SL * 416 + SL - 1:SL * 432:SL], 16, 0.0, ["woz1"])
-    fill(T.ew[:, 0:16], 16, 0.0, ["ewz"])
-    fill(T.acc[:], 32, 0.0, ["acc%d" % t for t in range(NP)])
-    fill(T.acc2[:], 32, 0.0, ["acb%d" % t for t in range(NP)])
-    fill(p1, 32, 0.0, ["p1"])
-    op("s", act(T.cl[:, 64:96], T.nn[:], ACT.Identity, bias=K - RB), R=["nn"], W=["cl2"])
-    f20, f100, f5 = T.cb[:, 0:32], T.cb[:, 32:64], T.cb[:, 64:96]
-    c = [T.cc[:, 32 * i:32 * i + 32] for i in range(8)]
-    op("v", ts(c[0], f20, -20.0, None, A.mult), R=["cb0"], W=["c0"])
-    op("v", ts(c[1], f100, -100.0, None, A.mult), R=["cb0"], W=["c1"])
-    op("v", ts(c[2], f100, 20.0, None, A.mult), R=["cb0"], W=["c2"])
-    op("v", tt(c[3], c[0], T.nn[:], A.add), R=["c0", "nn"], W=["c3"])
-    op("v", tt(T.cl[:, 32:64], c[1], T.nn[:], A.add), R=["c1", "nn"], W=["cl1"])
-    op("v", ts(col(6), odd, par, 432.0, A.not_equal, A.mult), R=["pc"], W=["pc6"])
-    op("v", ts(col(7), odd, par, 176.0, A.not_equal, A.mult), R=["pc"], W=["pc7"])
-    op("v", ts(col(9), jq, 5.0 * L, None, A.mult), R=["pc"], W=["pc9"])
-    op("v", ts(T.lh[:, 32:34], T.nn[:, 0:2], 16.0, col(6), A.mult, A.add), R=["nn", "pc6"], W=["lh2"])
-    op("v", quant(T.xq0[:], T.xs0[:], T.xin[:]), R=["xin0", "xin1"], W=["xq0"])
-    op("v", tt(T.cl[:, 0:32], c[2], c[3], A.add), R=["c2", "c3"], W=["cl0"])
-    op("v", cp(T.co[:, 32:64], T.cl[:, 32:64]), R=["cl1"], W=["coB"])
+    LA, LB, LB2, LC, LN, LM, LS, LE, LR, LP = 0, 32, 48, 66, 96, 122, 148, 150, 152, 184
+    listA, listB, listC = at("co", LA, LA + 32), [at("co", LB, LB + 15), at("co", LB2, LB2 + 17)], [at("co", LC, LC + 13), at("co", LC + 16, LC + 30)]
+    listN, listM, listS, listE, listR, listP = [at("co", a, a + n) for a, n in ((LN, NP), (LM, NP), (LS, 2), (LE, 2), (LR, 32), (LP, NP))]
 
-    def more_constants():
-        op("v", quant(T.eq[:], T.esc[:], T.et[:]), R=["et0", "et1", "et2", "et3"], W=["eq"])
-        op("g", iota(T.vcb[:, 0:NP], [[1023 * L, 5], [L, 5]], C, small=True), W=["vcb"])
-        op("v", ts(T.co[:, 0:32], T.cl[:, 0:32], 99.0, None, A.min), R=["cl0"], W=["coA"])
-        op("v", ts(T.ca[:, 64:96], c[3], 0.2, -0.4, A.mult, A.add), R=["c3"], W=["ca2"])
+    def term(a, n, k):
+        return at("terms", 4 * a + k, 4 * (a + n), 4)
 
-    def later_constants():
-        op("v", ts(c[4], f20, 160.0, h16, A.mult, A.add), R=["cb0", "pc"], W=["c4"])
-        op("v", cp(f5, T.ca[:, 64:96]), R=["ca2"], W=["cb2"])
-        op("v", ts(c[5], f100, -796.0, None, A.mult), R=["cb0"], W=["c5"])
-        op("v", ts(c[6], c[3], 32.0, None, A.mult), R=["c3"], W=["c6"])
-        op("v", ts(c[7], f5, -159.0, None, A.mult), R=["cb2"], W=["c7"])
-        op("v", tt(c[0], c[4], c[5], A.add), R=["c4", "c5"], W=["c0"])
-        op("v", tt(c[1], c[6], c[7], A.add), R=["c6", "c7"], W=["c1"])
-        op("v", cp(T.ro[:], T.ri[:]), R=["ri0", "ri1"], W=["ro"])
-        op("v", tt(T.cl[:, 96:128], c[0], c[1], A.add), R=["c0", "c1"], W=["cl3"])
-        op("v", ts(T.co[:, 64:96], f20, 32.0, 799.0, A.mult, A.min), R=["cb0"], W=["coR"])
-        op("v", cp(T.co[:, 96:122], T.cl[:, 96:122]), R=["cl3"], W=["coN"])
-        op("v", ts(T.dmask[:], T.qrow[:], q, None, A.is_equal), R=["qrow", "pc"], W=["dmask"])
-        op("v", ts(T.smask[:], T.qrow[:], q, None, A.is_gt), R=["qrow", "pc"], W=["smask"])
-        op("v", ts(T.pb[:, 6:7], T.pi[:], 4, None, A.logical_shift_right), R=["pi"], W=["gi"])
-        op("v", ts(T.lh[:, 36:38], T.nn[:, 0:2], 16.0, col(7), A.mult, A.add), R=["nn", "pc7"], W=["lh3"])
-        op("v", ts(T.cl[:, 128:160], f20, 5.0, None, A.mult), R=["cb0"], W=["m0"])
-        op("v", ts(T.cl[:, 160:192], f100, 75.0, None, A.mult), R=["cb0"], W=["m1"])
-        op("v", ts(T.cl[:, 192:224], f5, 20.0, None, A.mult), R=["cb2"], W=["m2"])
-        op("v", ts(col(8), iq, 5115.0 * L, col(9), A.mult, A.add), R=["pc", "pc9"], W=["pc8"])
-        op("v", tt(T.cl[:, 128:160], T.cl[:, 128:160], T.cl[:, 160:192], A.add), R=["m0", "m1"], W=["m0"])
-        op("v", tt(T.cl[:, 192:224], T.cl[:, 192:224], c[3], A.add), R=["m2", "c3"], W=["m2"])
-        op("v", ts(T.so[:, 0:2], T.lh[:, 32:34], 15.0, 831.0, A.add, A.min), R=["lh2"], W=["so"])
-        op("v", tt(T.cl[:, 224:256], T.cl[:, 128:160], T.cl[:, 192:224], A.add), R=["m0", "m2"], W=["m3"])
-        op("v", ts(T.so[:, 2:4], T.lh[:, 36:38], 351.0, None, A.min), R=["lh3"], W=["eo"])
-        op("v", cp(T.co[:, 128:154], T.cl[:, 224:250]), R=["m3"], W=["coM"])
+    def nn(a, z):
+        return at("nn", a, z)
 
-    listA, listB, listR, listN, listM = T.co[:, 0:32], T.co[:, 32:64], T.co[:, 64:96], T.co[:, 96:121], T.co[:, 128:153]
+    def f20(a, z):
+        return at("quo", a, z)
+
+    def f100(a, z):
+        return at("quo", 32 + a, 32 + z)
+
+    def f5(a, z):
+        return at("quo", 64 + a, 64 + z)
+
+    q, h16, iq, jq, odd, par, flip, i100, j100, ij, first, shifted, over, even, nq, nqh = [col(i) for i in range(16)]
+    k4 = at("km", 0, 4)
+    iota(at("pi"), [[0, 1]], 0, 1, False)
+    iota(at("n16"), [[16, 32]])
+    iota(at("ui"), [[1, 2], [16, 8]], small=False)
+    iota(k4, [[1, 4]])
+    mset(at("ones"), 1.0)
+    mset(at("terms", 0, 4 * LC), 0.0)
+    ones_where("et", [[1, 516]], A.is_equal, -3, -4)
+    ones_where("r4", [[0, 100], [1, 4]], A.not_equal)
+    ones_where("r20m", [[0, 26], [1, 20]], A.not_equal)
+    ts(at("pb", 0, 1), at("pi"), 15, None, A.bitwise_and)
+    ts(at("pb", 1, 2), at("pi"), 16, None, A.bitwise_and)
+    ts(at("pb", 2, 3), at("pi"), 2, 3, A.logical_shift_right, A.bitwise_and)
+    ts(at("pb", 3, 4), at("pi"), 3, None, A.bitwise_and)
+    ts(at("pb", 4, 5), at("pi"), 4, 1, A.logical_shift_right, A.bitwise_and)
+    ts(at("pb", 5, 6), at("pi"), 1, None, A.bitwise_and)
+    cp(at("uo"), at("ui"))
+    cp(col(0, 6), at("pb", 0, 6))
+    mset(at("terms", 4 * LC, 4 * LR), 0.0)
+    ts(at("km", 8, 12), k4, jq, None, A.is_equal)
+    ts(at("km", 4, 8), k4, iq, None, A.is_equal)
+    ts(flip, odd, par, 432.0, A.not_equal, A.mult)
+    for k in range(2):
+        ts(at("mjt", 100 * k, 100 * k + 100), at("ones", 0, 100), at("km", 8 + k, 9 + k), None, A.mult)
+    line(at("nn"), at("n16"), 1.0, q)
+    line(col(7, 2), col(2, 2), 5.0 * L)
+    line(first, q, -1.0, 16.0 * NB + 15)
+    line(f20(0, 32), at("nn"), 1.0 / 20, UP - 0.475)
+    line(f100(0, 32), at("nn"), 1.0 / 100, UP - 0.495)
+    line(term(LA, 32, 0), at("nn"), 4.0, 3.0)
+    line(term(LB, 16, 0), nn(0, 16), 1.0, 100 * UP)
+    line(term(LB2, 17, 0), nn(15, 32), 1.0, 100 * UP)
+    line(term(LA, 32, 1), f20(0, 32), -80.0)
+    line(term(LA, 32, 2), f100(0, 32), 80.0)
+    line(term(LB, 16, 1), f100(0, 16), -100.0)
+    line(term(LB2, 17, 1), f100(15, 32), -100.0)
+    line(f5(0, 32), at("nn"), 1.0 / 5, UP - 0.4)
+    quant(at("uq"), at("usc"), at("uin"))
+    cp(words(at("urq", 128, 256)), by(words(at("uq")), at("uo", 8, 16)))
+    act(at("ursc", 128, 256), by(at("usc"), at("uo", 8, 16)), ACT.Copy)
+    quant(at("xq0"), at("xs0"), at("xin"))
+    for b in range(4):
+        quant(at("eq", 128 * b, 128 * b + 128), at("esc", 128 * b, 128 * b + 128), at("et", 3 - b, 515 - b))
+    act(at("ursc", 0, 128), by(at("usc"), at("uo", 0, 8)), ACT.Copy)
+    line(term(LN, 26, 0), nn(0, 26), 32.0, h16)
+    line(term(LN, 26, 1), f20(0, 26), 156.0, UP * 799)
+    line(term(LN, 26, 2), f100(0, 26), -796.0)
+    line(term(LN, 26, 3), f5(0, 26), -159.0)
+    line(even, odd, -1.0, 1.0)
+
+    def kind(k):
+        return (T.vrep[k:128:16, :], [("vrep%d" % k, 1)])
+    vrep = (T.vrep[:], [("vrep%d" % k, 1) for k in range(4)])
+
+    def zeros(*views):
+        for name, a, z in views:
+            iota(at(name, a, z), [[0, z - a]])
+
+    def lists(a, z, upto):
+        scan(at("tsum", 4 * a, 4 * z), at("r4", 0, 4 * (z - a)), at("terms", 4 * a, 4 * z), A.mult, A.add)
+        cp(at("co", a, upto), at("tsum", 4 * a + 3, 4 * upto, 4))
+
+    def after_first_scores():
+        iota(at("seq", 0, 16), [[L, 8], [6 * L, 2]], -1)
+        iota(at("seq", 16, 32), [[L, 8], [7 * L, 2]], -1)
+        iota(at("tsum", 4 * LP + 3, 840, 4), [[16, 26]], 15)
+        zeros(("a0", C, C + 48), ("rmax", 512, 528), ("best", NP, 32))
+        iota(at("qrow"), [[0, 25], [1, 16]])
+        cp(words(at("urq", 0, 128)), by(words(at("uq")), at("uo", 0, 8)))
+        lists(0, LC, LC)
+
+    def later_terms():
+        line(term(LM, 26, 0), nn(0, 26), 1.0)
+        line(term(LM, 26, 1), f20(0, 26), -95.0)
+        line(term(LM, 26, 2), f100(0, 26), 75.0)
+        line(term(LM, 26, 3), f5(0, 26), 20.0)
+        line(at("quo", 96, 98), nn(0, 2), 1.0 / 2, UP - 0.25)
+        line(at("quo", 98, 100), nn(0, 2), 1.0 / 10, UP - 0.45)
+        line(term(LC, 30, 0), at("seq", 2, 32), even)
+        line(term(LC, 30, 1), at("seq", 1, 31), odd)
+        line(term(LS, 2, 0), nn(0, 2), 16.0, flip)
+        line(term(LS, 2, 1), nn(0, 2), 0.0, 15.0)
+        line(term(LE, 2, 0), nn(0, 2), 160.0, h16)
+        line(term(LE, 2, 1), at("quo", 96, 98), -288.0, UP * 447)
+        line(term(LE, 2, 2), at("quo", 98, 100), -159.0)
+        line(at("tsum", 4 * LR + 3, 4 * LP, 4), f20(0, 32), 1.0, -UP)
+
+    def after_first_codes():
+        iota(at("vcb", 0, 25), [[L, 5], [0, 5]])
+        iota(at("vcb", 32, 57), [[0, 5], [L, 5]])
+        iota(at("vcb", 64, 89), [[L, 5], [1, 5]])
+        iota(vrep, [[0, C]])
+        ones_where("r16", [[0, 26], [1, 16]], A.not_equal)
+        iota(slot(2 * SL - 1, 0, C), [[0, C]])
+        zeros(("pq", 0, 128))
+        for k in range(4, -1, -1):
+            iota(slot(SL + k, C, C + 32 * (k + 1)), [[0, 32 * (k + 1)]])
+        for k in range(4, -1, -1):
+            iota(slot(k, -32 * (5 - k), 0), [[0, 32 * (5 - k)]])
+        zeros(("cs", 0, 16), ("cs", 416, 432), ("ew", 0, 16), ("cseg", 832, 960))
+        lists(LC, LR, 210)
+        ts(at("r20a"), at("r20m", 0, 512), BIG, -BIG, A.mult, A.add)
+        ts(nq, q, -BIG, None, A.mult)
+        ts(nqh, q, 0.5, -BIG, A.add, A.mult)
+        ts(ij, jq, 5.0, i100, A.mult, A.add)
+        ts(at("cum", SL - 1, SL * (C + 8), SL), at("ones", 0, C + 8), 16.0, None, A.mult)
+
+    def first_round_masks():
+        act(at("pen"), at("qrow"), ACT.Relu, scale=BIG, bias=nq)
+        line(at("rst"), at("qrow"), BIG, nqh)
+        line(at("vcb", 0, NP), at("vcb", 0, NP), 1.0, i100)
+        line(at("vcb", 32, 32 + NP), at("vcb", 32, 32 + NP), 1.0, j100)
+        line(at("vcb", 64, 64 + NP), at("vcb", 64, 64 + NP), 1.0, ij)
+        dma("y", kind(2), at("vcb", 64, 64 + NP))
+
+    def first_round_columns():
+        line(shifted, first, 1.0, h16)
+        line(over, first, 1000.0, -1000.0 * (K - 1))
+        line(at("left", 0, NP), at("n16", 0, NP), 1.0, K - 16.0 * NB - 15)
+        line(at("left", 0, NP), at("left", 0, NP), 1.0, q)
+        line(at("left", 0, NP), at("left", 0, NP), 1.0, q)
+
+    def slot(s, a, z):
+        o = SL * (PAD + (s // SL) * C) + s % SL
+        return at("wv", o + SL * a, o + SL * (z - 1) + 1, SL)
+
+    def ends(k, a, z):
+        o = SL * (len(GROUPS) - k) + SL - 1
+        return at("cum", o + SL * a, o + SL * (z - 1) + 1, SL)
 
     def win(b, n):
-        return T.w32[:, WW * b + C + K - n:WW * b + C + K]
+        return at("w32", WW * b + C + K - n, WW * b + C + K)
 
     def plane(b):
-        op("s", act(win(b, C), bank(b, C), ACT.Identity, scale=32.0), W=["w%d" % b], P=["b%d" % b])
+        line(win(b, C), bank(b, C), 32.0)
 
-    def unpack(k, codes, scales, key):
+    def unpack(k, codes, scales):
         for b in range(4):
-            op("t", mm(k + b, C, T.eq[:, 128 * b:128 * b + 128], T.esc[:, 128 * b:128 * b + 128], codes, scales), R=["eq", key], W=["b%d" % (k + b)])
+            mm(k + b, C, at("eq", 128 * b, 128 * b + 128), at("esc", 128 * b, 128 * b + 128), codes, scales)
 
     for r in range(ROUNDS):
         dst = partners[r]
         wide = topo.mask(core, dst)
-        xq, xs, X = T["xq%d" % r], T["xs%d" % r], "xq%d" % r
-        out, land = T["out%d" % r], T["land%d" % r]
-        tq, tsc, lq, lsc = T["tq%d" % r], T["ts%d" % r], T["lq%d" % r], T["ls%d" % r]
+        xq, xs = "xq%d" % r, "xs%d" % r
+        out, land = at("out%d" % r), at("land%d" % r)
+        tq, tsc, lq, lsc = at("tq%d" % r), at("ts%d" % r), at("lq%d" % r), at("ls%d" % r)
 
         for h in (1, 0):
-            op("t", mm(4 + h, 200, T.urq[:, 128:256], T.ursc[:, 128:256], xq[:, 200 * h:200 * h + 200], xs[:, 200 * h:200 * h + 200]),
-               R=["urq", "ursc", X], W=["b%d" % (4 + h)])
-        op("t", mm(6, C, T.urq[:, 0:128], T.ursc[:, 0:128], xq[:], xs[:]), R=["urq", "ursc", X], W=["b6"])
+            mm(4 + h, 200, at("urq", 128, 256), at("ursc", 128, 256), at(xq, 200 * h, 200 * h + 200), at(xs, 200 * h, 200 * h + 200))
         for k in range(2):
-            op("v", ts(T.sel1[:, 100 * k:100 * k + 100], bank(4, 100, 100 * k), T.km[:, 8 + k:9 + k], None, A.mult), R=["mj"], W=["sel1%d" % k], P=["b4"])
-            op("s", act(T.sel1[:, 200 + 100 * k:300 + 100 * k], bank(5, 100, 100 * k), ACT.Identity, scale=T.km[:, 10 + k:11 + k]),
-               R=["mj"], W=["sel1%d" % (2 + k)], P=["b5"])
-        for k in range(2):
-            op("v", tt(T.sel1h[:, 100 * k:100 * k + 100], T.sel1[:, 100 * k:100 * k + 100], T.sel1[:, 200 + 100 * k:300 + 100 * k], A.add),
-               R=["sel1%d" % k, "sel1%d" % (2 + k)], W=["sel1h%d" % k])
-        op("v", tt(out[:], T.sel1h[:, 0:100], T.sel1h[:, 100:200], A.add), R=["sel1h0", "sel1h1"], W=["out%d" % r])
-        send(dst, land[:], out[:], "arrs%d" % r, common, ["out%d" % r])
-        writer["land%d" % r] = ("arrs%d" % r, engines_of(common))
-        count["arrs%d" % r] = engines_of(common)
+            line(at("sel1", 200 + 100 * k, 300 + 100 * k), bank(5, 100, 100 * k), at("km", 10 + k, 11 + k))
+        tt(at("sel1", 0, 200), bank(4, 200), at("mjt"), A.mult)
+        tt(at("sel1h"), at("sel1", 0, 200), at("sel1", 200, C), A.add)
+        tt(out, at("sel1h", 0, 100), at("sel1h", 100, 200), A.add)
+        send(dst, land, out, "arrs%d" % r, common)
+        arrives("arrs%d" % r, land)
 
+        unpack(0, at(xq), at(xs))
+        if r == 0:
+            after_first_scores()
+        mm(6, C, at("urq", 0, 128), at("ursc", 0, 128), at(xq), at(xs))
+        act(at("tt", 0, 4 * C, 4), bank(0, C), ACT.Copy)
+        cp(at("tt", 1, 4 * C, 4), bank(1, C))
+        if r == 0:
+            later_terms()
+            cp(at("tt", 2, 4 * C, 4), bank(2, C))
+        else:
+            act(at("tt", 2, 4 * C, 4), bank(2, C), ACT.Copy)
+        cp(at("tt", 3, 4 * C, 4), bank(3, C))
+        quant(tq, tsc, at("tt"))
+        send(dst, u8(lq), u8(tq), "arrc%d" % r, wide)
+        send(dst, lsc, tsc, "arrc%d" % r, wide)
+        arrives("arrc%d" % r, lq, lsc)
         for k in range(4):
-            op("s", act(T.sel0[:, 100 * k:100 * k + 100], bank(6, 100, 100 * k), ACT.Identity, scale=T.km[:, 4 + k:5 + k]),
-               R=["mi"], W=["sel0%d" % k], P=["b6"])
+            line(at("sel0", k, C, 4), bank(6, 100, 100 * k), at("km", 4 + k, 5 + k))
+        scan(at("a0", 0, C), at("r4"), at("sel0"), A.mult, A.add)
+        act(at("aexp"), by(at("a0"), listA), ACT.Copy)
         if r == 0:
-            more_constants()
-        unpack(0, xq[:], xs[:], X)
-        if r > 0:
-            op("v", cp(T.tt[:, 2:4 * C:4], bank(2, C)), W=["tt2"], P=["b2"])
-        op("v", tt(T.sel0h[:], T.sel0[:, 0:200], T.sel0[:, 200:400], A.add), R=["sel00", "sel01", "sel02", "sel03"], W=["sel0h"])
-        op("s", act(T.tt[:, 0:4 * C:4], bank(0, C), ACT.Copy), W=["tt0"], P=["b0"])
-        op("v", tt(T.a0[:], T.sel0h[:, 0:100], T.sel0h[:, 100:200], A.add), R=["sel0h"], W=["a0"])
-        op("s", act(T.aexp[:], T.a0[:].indirect(listA), ACT.Copy), R=["a0", "coA"], W=["aexp"])
-        if r == 0:
-            later_constants()
-            op("s", act(T.tt[:, 2:4 * C:4], bank(2, C), ACT.Copy), W=["tt2"], P=["b2"])
-        op("v", cp(T.tt[:, 3:4 * C:4], bank(3, C)), W=["tt3"], P=["b3"])
-        op("s", act(T.tt[:, 1:4 * C:4], bank(1, C), ACT.Copy), W=["tt1"], P=["b1"])
-        op("v", quant(tq[:], tsc[:], T.tt[:]), R=["tt0", "tt1", "tt2", "tt3"], W=["tq%d" % r])
-        send(dst, u8(lq[:]), u8(tq[:]), "arrc%d" % r, wide, ["tq%d" % r])
-        send(dst, lsc[:], tsc[:], "arrc%d" % r, wide, ["tq%d" % r])
-        writer["lq%d" % r] = ("arrc%d" % r, 2 * engines_of(wide))
-        count["arrc%d" % r] = 2 * engines_of(wide)
-        if r == 0:
-            for u in range(SL, NP):
-                fill(T.wv[:, SL * 16 * u + u - SL:SL * 16 * (u + 1):SL], 16, 0.0, ["wz%d" % u])
-            op("s", act(T.r13[:, 0:SL * CW:SL], T.r16[:, 0:CW], ACT.Identity, scale=0.0), R=["r16"], W=["r13", "ones"])
-            dma("y", u8(T.wq[:]), T.wc[:], R=["land0"], W=["wq"])
-            dma("y", T.wsc[:], T.ws[:], W=["wsc"])
-            dma("y", T.vin[:], T.v[:], W=["vin"])
+            after_first_codes()
+            first_round_masks()
+            dma("y", u8(at("wq")), hbm(T.wc[:]), [land])
+            dma("y", at("wsc"), hbm(T.ws[:]))
+            dma("y", at("vin"), hbm(T.v[:]))
         else:
             plane(0)
-            plane(2)
+            plane(1)
         if r == 1:
-            op("v", quant(T.vq[:], T.vsc[:], T.vin[:]), R=["vin"], W=["vq"])
+            quant(at("vq"), at("vsc"), at("vin"))
 
-        op("v", tt(T.sums[:], land[:].indirect(listB), T.aexp[:], A.add), R=["land%d" % r, "coB", "aexp"], W=["sums"])
-        op("v", scan(T.rmax[:], T.r20a[:], T.sums[:], A.add, A.max), R=["r20a", "sums"], W=["rmax"])
-        op("v", cp(T.brep[:, 0:256], T.rmax[:].indirect(T.ro[:, 0:16])), R=["rmax", "ro"], W=["brep0"])
-        op("s", act(T.brep[:, 256:512], T.rmax[:].indirect(T.ro[:, 16:32]), ACT.Copy), R=["rmax", "ro"], W=["brep1"])
-        op("s", act(T.brep[:, 512:800], T.rmax[:].indirect(T.ro[:, 32:50]), ACT.Copy), R=["rmax", "ro"], W=["brep2"])
-        for k, (a, z) in enumerate(((0, 256), (256, 512), (512, 800))):
-            op("v", turn(T.btr[:, a:z], T.brep[:, a:z]), R=["brep%d" % k], W=["btr%d" % k])
-        btr = ["btr0", "btr1", "btr2", "coN"]
+        for k, (a, z, o, n) in enumerate(((0, 240, 0, 208), (240, 512, 208, 224))):
+            tt(at("sums", a, z), by(land, listB[k]), at("aexp", a, z), A.add)
+            scan(at("rmax", a, z), at("r20a", a, z), at("sums", a, z), A.add, A.max)
+            act(at("brep", o, o + n), by(at("rmax", a, z + 16 * k), listC[k]), ACT.Copy)
+        act(at("best", 0, NP), at("rmax", 19, 500, 20), ACT.Copy)
+        turn(at("btr", 0, 192), at("brep", 0, 192))
+        turn(at("btr", 192, 384), at("brep", 16, 208))
+        turn(at("btr", 384, 608), at("brep", 208, 432))
+        turn(at("btr", 608, 800), at("brep", 224, 416))
+        plane(2)
+        act(at("row"), by(at("btr"), listN), ACT.Copy)
+        tt(at("rowz"), by(at("btr"), listN), at("pen"), A.subtract)
         plane(3)
-        op("s", act(T.row[:], T.btr[:].indirect(listN), ACT.Copy), R=btr, W=["row"])
-        op("v", tt(T.rowd[:], T.btr[:].indirect(listN), T.dmask[:], A.mult), R=btr + ["dmask"], W=["rowd"])
-        plane(1)
-        op("v", scan(T.piv[:], T.r16[:, 0:C], T.rowd[:], A.mult, A.add), R=["r16", "rowd"], W=["piv"])
+        scan(at("piv"), at("rst"), at("rowz"), A.min, A.max)
 
         def pivot(t):
-            return T.piv[:, 16 * t + 15:16 * t + 16]
-
-        def slots(t, a, z):
-            return T.wv[:, SL * a + t % SL:SL * z:SL]
+            return at("piv", 16 * t + 15, 16 * t + 16)
 
         def parts(t):
             a, z = 16 * (t + 1), 16 * (t + 1 + NB)
-            return ([(a, min(z, C), A.is_gt, "a")] if a < C else []) + ([(0, z - C, A.is_ge, "b")] if z > C else [])
+            return ([(a, min(z, C), A.is_gt, t % NB)] if a < C else []) + ([(0, z - C, A.is_ge, t - NB - 1)] if z > C else [])
 
-        def sign(t):
-            op("s", act(T.sg[:, 192 * t:192 * t + 192], T.row[:, 16 * t + 16:16 * t + 208], ACT.Sign, bias=pivot(t), scale=-1.0), R=["row", "piv"], W=["sg%d" % t])
+        def sign(i, job):
+            t, k, (a, z, o, s) = job
+            act(at("sg", 192 * (i % 4), 192 * (i % 4) + z - a), at("row", a, z), ACT.Sign, bias=pivot(t), scale=-1.0)
 
-        def keep(t):
-            op("s", act(slots(t, 16 * t + 16, 16 * t + 208), T.sg[:, 192 * t:192 * t + 192], ACT.Relu, scale=-1.0, accum_out=T.acc[:, t:t + 1]),
-               R=["sg%d" % t], W=["wa%d" % t, "acc%d" % t])
+        def keep(i, job):
+            t, k, (a, z, o, s) = job
+            signs, total = at("sg", 192 * (i % 4), 192 * (i % 4) + z - a), at("pq", 4 * t + k, 4 * t + k + 1)
+            if o == A.is_gt:
+                act(slot(s, a, z), signs, ACT.Relu, total, scale=-1.0)
+            else:
+                act(slot(s, a, z), signs, ACT.Sign, total, scale=-1.0, bias=1.0)
 
         def compare(t):
             for a, z, o, s in parts(t):
-                op("v", ts(slots(t, a, z), T.row[:, a:z], pivot(t), None, o), R=["row", "piv"], W=["w%s%d" % (s, t)])
+                ts(slot(s, a, z), at("row", a, z), pivot(t), None, o)
 
-        def tally(t, i):
-            a, z, o, s = parts(t)[i]
-            j = 192 * t + (0 if i == 0 else 192 - z)
-            op("s", act(T.junk[:, j:j + z - a], slots(t, a, z), ACT.Copy, accum_out=(T.acc2 if i else T.acc)[:, t:t + 1]),
-               R=["w%s%d" % (s, t)], W=["junk%d%d" % (i, t), ("acb%d" if i else "acc%d") % t])
+        def tally(t):
+            p = parts(t)
+            if len(p) == 1:
+                a, z, o, s = p[0]
+                n, d0, d1 = 96, slot(s, a, a + 96), slot(s, a + 96, z)
+            else:
+                n = max(p[0][1] - p[0][0], p[1][1])
+                d0, d1 = slot(p[0][3], p[0][0], p[0][0] + n), slot(p[1][3], p[1][1] - n, p[1][1])
+            e = 176 * (t - V0 + 1)
+            scan(at("junk", e - n, e), d0, d1, A.add, A.add)
 
         def columns(k):
-            a, z = CW * k, CW * k + CW
-            keys = ["w%s%d" % (p[3], t) for t in range(NP) for p in parts(t) if p[0] < z and p[1] > a]
-            op("v", scan(T.wo[:, SL * (16 + a):SL * (16 + z)], T.r13[:], T.wv[:, SL * a:SL * z], A.mult, A.add),
-               R=keys + ["r13", "wz"] + ["wz%d" % u for u in range(SL, NP)], W=["wo%d" % k])
+            a, z = 16 * GROUPS[k][0], 16 * GROUPS[k][1]
+            o = SL * (len(GROUPS) - k)
+            scan(at("cum", o + SL * a, o + SL * z), at("wv", SL * (PAD + a), SL * (PAD + z)), at("wv", SL * (PAD + C + a), SL * (PAD + C + z)), A.add, A.add, 16.0)
 
-        sign(0)
-        op("v", tt(T.lt[:], T.brep[:].indirect(listR), T.rmax[:], A.is_gt), R=["rmax", "brep0", "brep1", "brep2", "coR"], W=["lt"])
-        compare(NP - 1)
-        op("v", scan(T.mid[:], T.r20m[:], T.lt[:], A.mult, A.add), R=["r20m", "lt"], W=["mid"])
-        compare(NP - 2)
-        op("v", ts(T.vblk[:, 32:32 + NP], T.mid[:, 19:500:20], 1024.0, col(8), A.mult, A.add), R=["mid", "pc8"], W=["vb0"])
-        compare(NP - 3)
-        op("v", tt(T.vblk[:, 0:NP], T.vblk[:, 32:32 + NP], T.vcb[:, 0:NP], A.add), R=["vb0", "vcb"], W=["vblk"])
-        dma("y", T.tbl[:], T.vblk[:, 0:NP], R=["vblk"], W=["tbl"])
-        order("g", ["tbl", "gi"], ["vrep"], ())
-        g.indirect_dma_start(T.vrep[:], None, T.tbl[:], IndirectOffsetOnAxis(ap=T.pb[:, 6:7], axis=0), bounds_check=7).then_inc(T.sem.rows, 16)
-        count["rows"] = count.get("rows", 0) + 16
-        done(("rows", count["rows"]), ["tbl", "gi"], ["vrep"], ())
-        for t in range(NP - 4, NS - 1, -1):
+        def steps(k):
+            a, z = 16 * GROUPS[k][0], 16 * GROUPS[k][1]
+            scan(at("cs", 16 + a, 16 + z), ends(k, a, z), ends(k, a - 1, z - 1), A.max, A.subtract)
+
+        def across(a, z, shift):
+            o = 416 * shift
+            turn(at("ctr", o + a, o + z), at("cs", 16 - 16 * shift + a, 16 - 16 * shift + z))
+
+        def sixteen(a, z, shift):
+            o = 416 * shift
+            scan(at("cseg", o + a, o + z), at("r16", 0, z - a), at("ctr", o + a, o + z), A.mult, A.add)
+
+        by_s = list(range(V1, NP)) + list(range(V0 - 1, -1, -1))
+        by_v = list(range(V1 - 1, V0 - 1, -1))
+        jobs = [(t, k, p) for t in by_s for k, p in enumerate(parts(t))]
+        sign(0, jobs[0])
+        tt(at("lt"), by(at("best"), listR), at("rmax", 0, 512), A.is_gt)
+        compare(by_v[0])
+        scan(at("mid"), at("r20m", 0, 512), at("lt"), A.mult, A.add)
+        compare(by_v[1])
+        for k in range(2):
+            tt(at("vblk", 32 * k, 32 * k + NP), at("mid", 19, 500, 20), at("vcb", 32 * k, 32 * k + NP), A.add)
+            dma("y", kind(k), at("vblk", 32 * k, 32 * k + NP))
+        for i, job in enumerate(jobs):
+            if i + 1 < len(jobs):
+                sign(i + 1, jobs[i + 1])
+            keep(i, job)
+        tt(slot(NB, 0, C), by(at("piv"), listP), at("rowz"), A.is_le)
+        for t in by_v[2:]:
             compare(t)
-        for t in range(NS):
-            if t + 1 < NS:
-                sign(t + 1)
-            keep(t)
-        op("v", tt(T.dif[:], T.piv[:].indirect(T.ro[:, 50:75]), T.row[:], A.subtract), R=["piv", "ro", "row"], W=["dif"])
-        unpack(4, lq[:], lsc[:], "lq%d" % r)
-        for t in range(NS, NP):
-            if len(parts(t)) > 1:
-                tally(t, 1)
-        for t in range(NS, NP):
-            tally(t, 0)
-        op("s", act(T.vrow[:], T.vrep[:].indirect(listM), ACT.Copy), R=["vrep", "coM"], W=["vrow"])
-        columns(0)
-        op("v", ts(T.ged[:], T.dif[:], 0.0, None, A.is_le), R=["dif"], W=["ged"])
-        op("v", ts(T.eqd[:], T.dif[:], 0.0, None, A.is_equal), R=["dif"], W=["eqd"])
-        op("v", scan(T.ges[:], T.r16[:, 0:C], T.ged[:], A.mult, A.add), R=["ged", "r16"], W=["ges"])
-        op("v", scan(T.eqs[:], T.eqd[:], T.smask[:], A.add, A.mult), R=["eqd", "smask"], W=["eqs"])
+        unpack(4, lq, lsc)
+        scan(at("dsum"), at("r16", 0, C), slot(NB, 0, C), A.mult, A.add)
+        if EARLY:
+            columns(0)
+            tally(by_v[0])
+            steps(0)
+            tally(by_v[1])
+            across(256, 416, 0)
+            across(288, 416, 1)
+            sixteen(256, 416, 0)
+            sixteen(288, 416, 1)
+            for t in by_v[2:]:
+                tally(t)
+        else:
+            for t in by_v:
+                tally(t)
+            columns(0)
+        act(at("pq", 2, 4 * NP, 4), at("dsum", 15, C, 16), ACT.Copy)
+        act(at("pq", 4 * V0, 4 * V1, 4), at("junk", 175, 176 * (V1 - V0), 176), ACT.Copy)
+        act(at("vrow"), by(vrep, listM), ACT.Copy)
+        if r == 0:
+            first_round_columns()
         columns(1)
-        op("v", tt(T.pp[:, 0:NP], T.ges[:, 15:C:16], T.eqs[:, 15:C:16], A.subtract), R=["ges", "eqs"], W=["p1"])
-        for k in range(2, C // CW):
-            columns(k)
-        wo = ["wo%d" % k for k in range(C // CW)] + ["woz0", "woz1"]
-        op("v", tt(p2, p1, T.acc2[:], A.add), R=["p1"] + ["acb%d" % t for t in range(NP)], W=["p2"])
-        op("v", turn(T.ctr[:, 0:416], T.wo[:, SL * 16 + SL - 1:SL * 432:SL]), R=wo, W=["ctr0"])
-        op("v", turn(T.ctr[:, 416:832], T.wo[:, SL - 1:SL * 416:SL]), R=wo, W=["ctr1"])
-        op("v", scan(T.cseg[:], T.r16[:], T.ctr[:], A.mult, A.add), R=["r16", "ctr0", "ctr1"], W=["cseg"])
-        op("v", tt(p3, p2, T.acc[:], A.add), R=["p2"] + ["acc%d" % t for t in range(NP)], W=["p3"])
-        op("v", tt(T.nrk[:], T.cseg[:].indirect(T.so[:, 0:2]), p3, A.subtract), R=["cseg", "so", "p3"], W=["nrk"])
-        op("v", ts(T.rko[:, 0:NP], T.nrk[:, 0:NP], -1.0, RB + 16.0, A.mult, A.add), R=["nrk"], W=["rko"])
-        op("s", act(T.xa[:, 0:NP], T.nrk[:, 0:NP], ACT.Relu, scale=-1000.0, bias=1000.0 * (RB - K + 1)), R=["nrk"], W=["xa0"])
+        if not EARLY:
+            steps(0)
+        columns(2)
+        steps(1)
+        steps(2)
+        scan(at("pp"), at("r4", 0, 128), at("pq"), A.mult, A.add)
+        a0, a1 = (256, 288) if EARLY else (416, 416)
+        across(0, a0, 0)
+        across(0, a1, 1)
+        sixteen(0, a0, 0)
+        sixteen(0, a1, 1)
+        tt(at("nrk"), by(at("cseg"), listS), at("pp", 3, 128, 4), A.subtract)
+        ts(at("rko", 0, NP), at("nrk", 0, NP), -1.0, shifted, A.mult, A.add)
+        for b in range(4):
+            line(at("tb", C * b, C * b + C), bank(4 + b, C), 0.5)
         if r == 0:
             plane(0)
-            plane(2)
+            plane(1)
+        act(at("xa", 0, NP), at("nrk", 0, NP), ACT.Relu, scale=-1000.0, bias=over)
+        scatter(at("ew"), at("rko", 0, NP), at("vrow"))
+        turn(at("etr", 0, K), at("ew", 0, K))
+        turn(at("etr", K, 2 * K), at("ew", 16, K + 16))
+        cp(at("lst"), by(at("etr"), listE))
+        la, lo, le = at("lst", 0, 10), at("lst", 10, 20), at("lst", 20, 30)
         for b in range(4):
-            op("s", act(T.tb[:, C * b:C * b + C], bank(4 + b, C), ACT.Identity, scale=0.5), W=["tb%d" % b], P=["b%d" % (4 + b)])
-        op("v", cp(T.ew[:].indirect(T.rko[:, 0:NP]), T.vrow[:]), R=["vrow", "rko", "ewz"], W=["ew"])
-        op("v", turn(T.etr[:, 0:K], T.ew[:, 16:K + 16]), R=["ew"], W=["etr0"])
-        op("v", turn(T.etr[:, K:352], T.ew[:, 0:192]), R=["ew"], W=["etr1"])
-        op("v", cp(T.li[:, 0:16], T.etr[:].indirect(T.so[:, 2:3])), R=["etr0", "etr1", "eo"], W=["li"])
-        la, ld = T.lj[:, 0:10], T.lb[:, 0:10]
-        op("v", ts(la, T.li[:, 0:10], 10, None, A.logical_shift_right), R=["li"], W=["lj0"])
-        op("v", ts(ld, T.li[:, 0:10], 1023, None, A.bitwise_and), R=["li"], W=["lj1"])
-        op("v", cp(T.la[:, 0:10], la), R=["lj0"], W=["la"])
-        op("v", tt(T.lj[:, 10:20], la, ld, A.add), R=["lj0", "lj1"], W=["lb"])
-        op("v", ts(T.lo[:, 0:10], T.lj[:, 10:20], -float(C), None, A.add), R=["lb"], W=["lo"])
-        op("v", ts(T.lf[:, 0:20], T.lj[:, 0:20], 0.05, -0.475, A.mult, A.add), R=["lj0", "lb"], W=["lf0"])
+            line(at("ah", K * b, K * b + K), by(win(b, C), la), 2.0 ** -6)
+        xa = [at("xa", 32 * i, 32 * i + NP) for i in range(3)]
+        tt(xa[1], xa[0], at("nrk", 0, NP), A.subtract)
+        tt(xa[2], xa[1], at("left", 0, NP), A.min)
         for b in range(4):
-            op("s", act(T.ah[:, K * b:K * b + K], win(b, C).indirect(T.la[:, 0:10]), ACT.Identity, scale=2.0 ** -6), R=["w%d" % b, "la"], W=["ah%d" % b])
-        op("v", cp(T.lg[:, 0:20], T.lf[:, 0:20]), R=["lf0"], W=["lg"])
-
-        def zpart(b):
-            op("v", tt(T.zt[:, b:4 * K:4], T.tb[:, C * b:C * b + C].indirect(T.lo[:, 0:10]), T.ah[:, K * b:K * b + K], A.add),
-               R=["tb%d" % b, "lo", "ah%d" % b], W=["zt%d" % b])
-        zpart(0)
-        op("v", ts(T.lh[:, 0:10], T.lg[:, 0:10], 20.0, -20.0, A.mult, A.add), R=["lg"], W=["lh0"])
-        zpart(1)
-        op("v", tt(T.lh[:, 16:26], T.lh[:, 0:10], T.lg[:, 10:20], A.add), R=["lh0", "lg"], W=["lh1"])
-        op("v", cp(T.le[:, 0:10], T.lh[:, 16:26]), R=["lh1"], W=["le"])
-        zpart(2)
-        zpart(3)
+            tt(at("zt", b, 4 * K, 4), by(at("tb", C * b, C * b + C), lo), at("ah", K * b, K * b + K), A.add)
         for b in range(4):
-            op("s", act(T.te[:, K * b:K * b + K], win(b, C).indirect(T.le[:, 0:10]), ACT.Copy), R=["w%d" % b, "le"], W=["te%d" % b])
-        op("v", quant(T.zq[:], T.zsc[:], T.zt[:]), R=["zt0", "zt1", "zt2", "zt3"], W=["zq"])
+            act(at("te", K * b, K * b + K), by(win(b, C), le), ACT.Copy)
+        quant(at("zq"), at("zsc"), at("zt"))
+        ts(at("xo", 0, NP), xa[2], first, None, A.add)
         for b in range(4):
-            op("t", mm(4 + b, K, T.wq[:, 128 * b:128 * b + 128], T.wsc[:, 128 * b:128 * b + 128], T.zq[:], T.zsc[:]),
-               R=["wq", "wsc", "zq"], W=["b%d" % (4 + b)])
-        xa = [T.xa[:, 32 * i:32 * i + NP] for i in range(3)]
-        op("v", tt(xa[1], xa[0], T.nrk[:, 0:NP], A.subtract), R=["nrk", "xa0"], W=["xa1"])
-        op("v", tt(xa[2], xa[1], T.cl[:, 64:64 + NP], A.min), R=["xa1", "cl2"], W=["xa2"])
-        op("v", ts(T.xo[:, 0:NP], xa[2], RB, None, A.add), R=["xa2"], W=["xo"])
+            mm(4 + b, K, at("wq", 128 * b, 128 * b + 128), at("wsc", 128 * b, 128 * b + 128), at("zq"), at("zsc"))
         for b in range(4):
-            op("v", tt(T.w32[:, WW * b:WW * b + K], bank(4 + b, K), T.te[:, K * b:K * b + K], A.add),
-               R=["te%d" % b], W=["n%d" % b], P=["b%d" % (4 + b)])
+            tt(at("w32", WW * b, WW * b + K), bank(4 + b, K), at("te", K * b, K * b + K), A.add)
         for b, a, z, e in ((0, 0, NP, "s"), (3, 0, NP, "v"), (1, 0, NP, "s"), (2, 12, NP, "v"), (2, 0, 12, "s")):
-            o, w = T.xt[:, 64 * a + b:64 * z:4], win(b, C + K).indirect(T.xo[:, a:z])
-            call = act(o, w, ACT.Identity, scale=2.0 ** -5) if e == "s" else ts(o, w, 2.0 ** -5, None, A.mult)
-            op(e, call, R=["w%d" % b, "n%d" % b, "xo"], W=["xt%d%s" % (b, e)])
-        op("v", quant(T["xq%d" % (r + 1)][:], T["xs%d" % (r + 1)][:], T.xt[:]), R=["xt0s", "xt1s", "xt2s", "xt2v", "xt3v"], W=["xq%d" % (r + 1)])
+            o, w = at("xt", 64 * a + b, 64 * z, 4), by(win(b, C + K), at("xo", a, z))
+            if e == "s":
+                line(o, w, 2.0 ** -5)
+            else:
+                ts(o, w, 2.0 ** -5, None, A.mult)
+        quant(at("xq%d" % (r + 1)), at("xs%d" % (r + 1)), at("xt"))
 
-    xq, xs, X = T["xq%d" % ROUNDS], T["xs%d" % ROUNDS], "xq%d" % ROUNDS
+    xq, xs = "xq%d" % ROUNDS, "xs%d" % ROUNDS
     for h in (1, 0):
-        op("t", mm(h, 200, T.vq[:], T.vsc[:], xq[:, 200 * h:200 * h + 200], xs[:, 200 * h:200 * h + 200]), R=["vq", X], W=["b%d" % h])
-    dma("y", T.oc[:], u8(xq[:]), R=[X])
-    op("v", cp(T.yo[:, 0:200], bank(0, 200)), W=["yo0"], P=["b0"])
-    op("s", act(T.yo[:, 200:400], bank(1, 200), ACT.Copy), W=["yo1"], P=["b1"])
-    dma("y", T.osc[0:4, :], xs[0:4, :], R=[X])
-    dma("y", T.y[:, 0:200], T.yo[:, 0:200], R=["yo0"])
-    dma("s", T.y[:, 200:400], T.yo[:, 200:400], R=["yo1"])
-    dma("y", T.osc[4:8, :], xs[32:36, :], R=[X])
-    dma("s", T.osc[8:12, :], xs[64:68, :], R=[X])
-    dma("s", T.osc[12:16, :], xs[96:100, :], R=[X])
+        mm(h, 200, at("vq"), at("vsc"), at(xq, 200 * h, 200 * h + 200), at(xs, 200 * h, 200 * h + 200))
+
+    def scales(k):
+        return hbm(T.osc[4 * k:4 * k + 4, :]), (T[xs][32 * k:32 * k + 4, :], at(xs)[1])
+    dma("y", hbm(T.oc[:]), u8(at(xq)))
+    cp(at("yo", 0, 200), bank(0, 200))
+    act(at("yo", 200, C), bank(1, 200), ACT.Copy)
+    dma("y", *scales(0))
+    dma("y", hbm(T.y[:, 0:200]), at("yo", 0, 200))
+    dma("s", hbm(T.y[:, 200:400]), at("yo", 200, C))
+    dma("y", *scales(1))
+    dma("s", *scales(2))
+    dma("s", *scales(3))
     need("g", list(count.items()))

@@ -4,8 +4,16 @@ C, L, K, ROUNDS = 400, 20, 160, 3
 MASKS = [1, 2, 3]
 NP = 25
 NB = 12
-V0, V1 = 13, 24
+V0, V1 = 13, 25
 EARLY = 0
+WRAPS = []
+TALLY = 11
+OWN = 1
+WIDE = 1
+T1 = 23
+PL = 3
+CUT = 12
+MID = (3, 5, 4)
 SL = 7
 PAD = 160
 GROUPS = [(16, 25), (8, 16), (0, 8)]
@@ -16,12 +24,12 @@ UP = 136.0
 F32, BF, F16, I32, U16, X4, U8 = "float32", "bfloat16", "float16", "int32", "uint16", "float8_e4m3fn_x4", "uint8"
 SCRATCH = {"ps": ("psum", [128, 4096], F32)}
 for _d, _l in (
-    (BF, dict(xin=4 * C, uin=512, vin=512, et=516, ones=520, quo=128, qrow=C, pen=C, rst=C, r20m=520, r16=416, r4=C, mjt=200, lt=512, mid=512,
-              wv=2 * SL * (PAD + C), dsum=C, junk=176 * 16, sg=4 * 192, cs=432, ctr=832, cseg=960,
+    (BF, dict(xin=4 * C, uin=512, vin=512, et=516, ones=520, quo=128, qrow=C, pen=C, rst=C, r20m=520, r16=832, r4=C, mjt=200, lt=272, mid=272,
+              wv=2 * SL * (PAD + C), dsum=208, junk=176 * 16, sg=4 * 192, cs=432, ctr=832, cseg=960,
               tt=4 * C, w32=4 * WW, tb=4 * C, ah=4 * K, te=4 * K, zt=4 * K, xt=4 * C)),
     (F16, dict(cum=SL * (C + 8))),
     (F32, dict(pc=20, km=12, n16=32, nn=32, left=32, terms=608, tsum=840, r20a=512, sel1=C, sel1h=200, sel0=C, a0=C + 48,
-               aexp=512, sums=512, rmax=528, best=32, brep=432, btr=800, row=C, rowz=C, piv=C, pq=128, pp=128, nrk=32, seq=32,
+               aexp=512, sums=512, rmax=528, best=32, midf=32, brep=432, btr=800, row=C, rowz=C, piv=C, pq=128, pp=128, nrk=32, seq=32,
                vblk=64, vcb=96, vrep=C, vrow=C, ew=C + 16, etr=2 * K, xa=96, yo=C,
                out0=100, out1=100, out2=100, land0=100, land1=100, land2=100)),
     (I32, dict(pi=1, pb=8, ui=16)),
@@ -175,8 +183,9 @@ def rank_program(g, core, T, topo):
         else:
             op("g", lambda: g.iota(out[0], pattern, base, cm), [out], [])
 
-    def ones_where(name, pattern, compare, base=0, cm=0):
-        out, one = at(name), at("ones", 0, SCRATCH[name][1][1])
+    def ones_where(name, pattern, compare, base=0, cm=0, a=0, n=None):
+        n = n or SCRATCH[name][1][1]
+        out, one = at(name, a, a + n), at("ones", 0, n)
         op("g", lambda: g.affine_select(out[0], one[0], pattern, compare, 0.0, base, cm), [out], [one])
 
     def mm(k, n, lq, ls, rq, rs):
@@ -192,12 +201,12 @@ def rank_program(g, core, T, topo):
         common &= topo.mask(core, d)
 
     dma("s", at("uin"), hbm(T.u[:]))
-    dma("y", at("xin", 0, 800), hbm(T.x[:, 0:800]))
-    dma("s", at("xin", 800, 1600), hbm(T.x[:, 800:1600]))
+    dma("y", at("xin", 800, 1600), hbm(T.x[:, 800:1600]))
+    dma("s", at("xin", 0, 800), hbm(T.x[:, 0:800]))
 
-    LA, LB, LB2, LC, LN, LM, LS, LE, LR, LP = 0, 32, 48, 66, 96, 122, 148, 150, 152, 184
+    LA, LB, LB2, LC, LN, LM, LS, LE, LR, LV, LP = 0, 32, 48, 66, 96, 122, 148, 150, 152, 170, 174
     listA, listB, listC = at("co", LA, LA + 32), [at("co", LB, LB + 15), at("co", LB2, LB2 + 17)], [at("co", LC, LC + 13), at("co", LC + 16, LC + 30)]
-    listN, listM, listS, listE, listR, listP = [at("co", a, a + n) for a, n in ((LN, NP), (LM, NP), (LS, 2), (LE, 2), (LR, 32), (LP, NP))]
+    listN, listM, listS, listE, listR, listV, listP = [at("co", a, a + n) for a, n in ((LN, NP), (LM, NP), (LS, 2), (LE, 2), (LR, 17), (LV, 4), (LP, NP))]
 
     def term(a, n, k):
         return at("terms", 4 * a + k, 4 * (a + n), 4)
@@ -224,7 +233,11 @@ def rank_program(g, core, T, topo):
     mset(at("terms", 0, 4 * LC), 0.0)
     ones_where("et", [[1, 516]], A.is_equal, -3, -4)
     ones_where("r4", [[0, 100], [1, 4]], A.not_equal)
+    iota(at("seq", 0, 16), [[L, 8], [6 * L, 2]], -1)
+    iota(at("seq", 16, 32), [[L, 8], [7 * L, 2]], -1)
     ones_where("r20m", [[0, 26], [1, 20]], A.not_equal)
+    iota(at("tsum", 4 * LP + 3, 800, 4), [[16, 26]], 15)
+    iota(at("a0", C, C + 48), [[0, 48]])
     ts(at("pb", 0, 1), at("pi"), 15, None, A.bitwise_and)
     ts(at("pb", 1, 2), at("pi"), 16, None, A.bitwise_and)
     ts(at("pb", 2, 3), at("pi"), 2, 3, A.logical_shift_right, A.bitwise_and)
@@ -238,7 +251,7 @@ def rank_program(g, core, T, topo):
     ts(at("km", 4, 8), k4, iq, None, A.is_equal)
     ts(flip, odd, par, 432.0, A.not_equal, A.mult)
     for k in range(2):
-        ts(at("mjt", 100 * k, 100 * k + 100), at("ones", 0, 100), at("km", 8 + k, 9 + k), None, A.mult)
+        ts(at("mjt", 100 * k, 100 * k + 100), at("ones", 0, 100), at("km", 10 + k, 11 + k), None, A.mult)
     line(at("nn"), at("n16"), 1.0, q)
     line(col(7, 2), col(2, 2), 5.0 * L)
     line(first, q, -1.0, 16.0 * NB + 15)
@@ -255,15 +268,14 @@ def rank_program(g, core, T, topo):
     quant(at("uq"), at("usc"), at("uin"))
     cp(words(at("urq", 128, 256)), by(words(at("uq")), at("uo", 8, 16)))
     act(at("ursc", 128, 256), by(at("usc"), at("uo", 8, 16)), ACT.Copy)
-    quant(at("xq0"), at("xs0"), at("xin"))
-    for b in range(4):
-        quant(at("eq", 128 * b, 128 * b + 128), at("esc", 128 * b, 128 * b + 128), at("et", 3 - b, 515 - b))
+    for a in (200, 0):
+        quant(at("xq0", a, a + 200), at("xs0", a, a + 200), at("xin", 4 * a, 4 * a + 800))
+    cp(words(at("urq", 0, 128)), by(words(at("uq")), at("uo", 0, 8)))
     act(at("ursc", 0, 128), by(at("usc"), at("uo", 0, 8)), ACT.Copy)
-    line(term(LN, 26, 0), nn(0, 26), 32.0, h16)
-    line(term(LN, 26, 1), f20(0, 26), 156.0, UP * 799)
-    line(term(LN, 26, 2), f100(0, 26), -796.0)
-    line(term(LN, 26, 3), f5(0, 26), -159.0)
-    line(even, odd, -1.0, 1.0)
+    ts(even, odd, -1.0, 1.0, A.mult, A.add)
+    ts(nq, q, -BIG, None, A.mult)
+    ts(nqh, q, 0.5, -BIG, A.add, A.mult)
+    ts(ij, jq, 5.0, i100, A.mult, A.add)
 
     def kind(k):
         return (T.vrep[k:128:16, :], [("vrep%d" % k, 1)])
@@ -278,15 +290,20 @@ def rank_program(g, core, T, topo):
         cp(at("co", a, upto), at("tsum", 4 * a + 3, 4 * upto, 4))
 
     def after_first_scores():
-        iota(at("seq", 0, 16), [[L, 8], [6 * L, 2]], -1)
-        iota(at("seq", 16, 32), [[L, 8], [7 * L, 2]], -1)
-        iota(at("tsum", 4 * LP + 3, 840, 4), [[16, 26]], 15)
-        zeros(("a0", C, C + 48), ("rmax", 512, 528), ("best", NP, 32))
         iota(at("qrow"), [[0, 25], [1, 16]])
-        cp(words(at("urq", 0, 128)), by(words(at("uq")), at("uo", 0, 8)))
+        zeros(("rmax", 512, 528), ("best", NP, 32))
+        iota(at("vcb", 0, 25), [[L, 5], [0, 5]])
+        iota(at("vcb", 32, 57), [[0, 5], [L, 5]])
+        iota(at("vcb", 64, 89), [[L, 5], [1, 5]])
+        for b in range(4):
+            quant(at("eq", 128 * b, 128 * b + 128), at("esc", 128 * b, 128 * b + 128), at("et", 3 - b, 515 - b))
         lists(0, LC, LC)
 
     def later_terms():
+        line(term(LN, 26, 0), nn(0, 26), 32.0, h16)
+        line(term(LN, 26, 1), f20(0, 26), 156.0, UP * 799)
+        line(term(LN, 26, 2), f100(0, 26), -796.0)
+        line(term(LN, 26, 3), f5(0, 26), -159.0)
         line(term(LM, 26, 0), nn(0, 26), 1.0)
         line(term(LM, 26, 1), f20(0, 26), -95.0)
         line(term(LM, 26, 2), f100(0, 26), 75.0)
@@ -300,14 +317,17 @@ def rank_program(g, core, T, topo):
         line(term(LE, 2, 0), nn(0, 2), 160.0, h16)
         line(term(LE, 2, 1), at("quo", 96, 98), -288.0, UP * 447)
         line(term(LE, 2, 2), at("quo", 98, 100), -159.0)
-        line(at("tsum", 4 * LR + 3, 4 * LP, 4), f20(0, 32), 1.0, -UP)
+        line(at("tsum", 4 * LR + 3, 4 * LV, 4), f20(15, 33), 1.0, -UP)
+        for a in (LV, LV + 2):
+            line(at("tsum", 4 * a + 3, 4 * a + 8, 4), nn(0, 2), 1.0)
 
     def after_first_codes():
-        iota(at("vcb", 0, 25), [[L, 5], [0, 5]])
-        iota(at("vcb", 32, 57), [[0, 5], [L, 5]])
-        iota(at("vcb", 64, 89), [[L, 5], [1, 5]])
+        zeros(("vcb", NP, 32), ("vcb", 32 + NP, 64))
         iota(vrep, [[0, C]])
-        ones_where("r16", [[0, 26], [1, 16]], A.not_equal)
+        zeros(("midf", NP, 32))
+        iota(at("dsum", 7, 8), [[0, 1]], -200)
+        for a in (0, 416):
+            ones_where("r16", [[0, 26], [1, 16]], A.not_equal, a=a, n=416)
         iota(slot(2 * SL - 1, 0, C), [[0, C]])
         zeros(("pq", 0, 128))
         for k in range(4, -1, -1):
@@ -315,12 +335,7 @@ def rank_program(g, core, T, topo):
         for k in range(4, -1, -1):
             iota(slot(k, -32 * (5 - k), 0), [[0, 32 * (5 - k)]])
         zeros(("cs", 0, 16), ("cs", 416, 432), ("ew", 0, 16), ("cseg", 832, 960))
-        lists(LC, LR, 210)
-        ts(at("r20a"), at("r20m", 0, 512), BIG, -BIG, A.mult, A.add)
-        ts(nq, q, -BIG, None, A.mult)
-        ts(nqh, q, 0.5, -BIG, A.add, A.mult)
-        ts(ij, jq, 5.0, i100, A.mult, A.add)
-        ts(at("cum", SL - 1, SL * (C + 8), SL), at("ones", 0, C + 8), 16.0, None, A.mult)
+        zeros(("wv", SL * (PAD - 1), SL * PAD))
 
     def first_round_masks():
         act(at("pen"), at("qrow"), ACT.Relu, scale=BIG, bias=nq)
@@ -365,58 +380,65 @@ def rank_program(g, core, T, topo):
         for h in (1, 0):
             mm(4 + h, 200, at("urq", 128, 256), at("ursc", 128, 256), at(xq, 200 * h, 200 * h + 200), at(xs, 200 * h, 200 * h + 200))
         for k in range(2):
-            line(at("sel1", 200 + 100 * k, 300 + 100 * k), bank(5, 100, 100 * k), at("km", 10 + k, 11 + k))
-        tt(at("sel1", 0, 200), bank(4, 200), at("mjt"), A.mult)
-        tt(at("sel1h"), at("sel1", 0, 200), at("sel1", 200, C), A.add)
-        tt(out, at("sel1h", 0, 100), at("sel1h", 100, 200), A.add)
-        send(dst, land, out, "arrs%d" % r, common)
+            line(at("sel1", 100 * k, 100 + 100 * k), bank(4, 100, 100 * k), at("km", 8 + k, 9 + k))
+        tt(at("sel1", 200, C), bank(5, 200), at("mjt"), A.mult)
+        tt(at("sel1h", 0, 100), at("sel1", 200, 300), at("sel1", 300, C), A.add)
+        tt(at("sel1h", 100, 200), at("sel1h", 0, 100), at("sel1", 0, 100), A.add)
+        tt(out, at("sel1h", 100, 200), at("sel1", 100, 200), A.add)
+        send(dst, land, out, "arrs%d" % r, wide if WIDE else common)
         arrives("arrs%d" % r, land)
 
-        unpack(0, at(xq), at(xs))
+        mm(6, C, at("urq", 0, 128), at("ursc", 0, 128), at(xq), at(xs))
         if r == 0:
             after_first_scores()
-        mm(6, C, at("urq", 0, 128), at("ursc", 0, 128), at(xq), at(xs))
-        act(at("tt", 0, 4 * C, 4), bank(0, C), ACT.Copy)
-        cp(at("tt", 1, 4 * C, 4), bank(1, C))
+        unpack(0, at(xq), at(xs))
+        for k in range(4):
+            line(at("sel0", k, C, 4), bank(6, 100, 100 * k), at("km", 4 + k, 5 + k))
+        scan(at("a0", 0, C), at("r4"), at("sel0"), A.mult, A.add)
         if r == 0:
             later_terms()
-            cp(at("tt", 2, 4 * C, 4), bank(2, C))
-        else:
-            act(at("tt", 2, 4 * C, 4), bank(2, C), ACT.Copy)
-        cp(at("tt", 3, 4 * C, 4), bank(3, C))
+        act(at("tt", 0, 4 * C, 4), bank(0, C), ACT.Copy)
+        act(at("aexp"), by(at("a0"), listA), ACT.Copy)
+        if r == 0:
+            line(at("r20a"), at("r20m", 0, 512), BIG, -BIG)
+            lists(LC, LR, 200)
+        for b in range(1, 4):
+            cp(at("tt", b, 4 * C, 4), bank(b, C))
         quant(tq, tsc, at("tt"))
         send(dst, u8(lq), u8(tq), "arrc%d" % r, wide)
         send(dst, lsc, tsc, "arrc%d" % r, wide)
         arrives("arrc%d" % r, lq, lsc)
-        for k in range(4):
-            line(at("sel0", k, C, 4), bank(6, 100, 100 * k), at("km", 4 + k, 5 + k))
-        scan(at("a0", 0, C), at("r4"), at("sel0"), A.mult, A.add)
-        act(at("aexp"), by(at("a0"), listA), ACT.Copy)
         if r == 0:
             after_first_codes()
             first_round_masks()
             dma("y", u8(at("wq")), hbm(T.wc[:]), [land])
             dma("y", at("wsc"), hbm(T.ws[:]))
             dma("y", at("vin"), hbm(T.v[:]))
-        else:
-            plane(0)
-            plane(1)
+        for b in range(PL if r else 1):
+            plane(b)
         if r == 1:
             quant(at("vq"), at("vsc"), at("vin"))
+
+        def middles(a, n):
+            for u in range(a, a + n):
+                act(at("sg", L * u, L * u + L), at("rmax", L * u, L * u + L), ACT.Sign, at("midf", u, u + 1), scale=-1.0,
+                    bias=at("rmax", L * u + L - 1, L * u + L))
 
         for k, (a, z, o, n) in enumerate(((0, 240, 0, 208), (240, 512, 208, 224))):
             tt(at("sums", a, z), by(land, listB[k]), at("aexp", a, z), A.add)
             scan(at("rmax", a, z), at("r20a", a, z), at("sums", a, z), A.add, A.max)
             act(at("brep", o, o + n), by(at("rmax", a, z + 16 * k), listC[k]), ACT.Copy)
+            if k == 0:
+                middles(0, MID[0])
         act(at("best", 0, NP), at("rmax", 19, 500, 20), ACT.Copy)
         turn(at("btr", 0, 192), at("brep", 0, 192))
         turn(at("btr", 192, 384), at("brep", 16, 208))
         turn(at("btr", 384, 608), at("brep", 208, 432))
         turn(at("btr", 608, 800), at("brep", 224, 416))
-        plane(2)
+        middles(MID[0], MID[1])
         act(at("row"), by(at("btr"), listN), ACT.Copy)
         tt(at("rowz"), by(at("btr"), listN), at("pen"), A.subtract)
-        plane(3)
+        middles(MID[0] + MID[1], MID[2])
         scan(at("piv"), at("rst"), at("rowz"), A.min, A.max)
 
         def pivot(t):
@@ -438,15 +460,19 @@ def rank_program(g, core, T, topo):
             else:
                 act(slot(s, a, z), signs, ACT.Sign, total, scale=-1.0, bias=1.0)
 
+        def mine(t):
+            return parts(t)[:1] if t in WRAPS else parts(t)
+
         def compare(t):
-            for a, z, o, s in parts(t):
+            for a, z, o, s in mine(t):
                 ts(slot(s, a, z), at("row", a, z), pivot(t), None, o)
 
         def tally(t):
-            p = parts(t)
+            p = mine(t)
             if len(p) == 1:
                 a, z, o, s = p[0]
-                n, d0, d1 = 96, slot(s, a, a + 96), slot(s, a + 96, z)
+                n = (z - a) // 2
+                d0, d1 = slot(s, a, a + n), slot(s, a + n, z)
             else:
                 n = max(p[0][1] - p[0][0], p[1][1])
                 d0, d1 = slot(p[0][3], p[0][0], p[0][0] + n), slot(p[1][3], p[1][1] - n, p[1][1])
@@ -456,6 +482,7 @@ def rank_program(g, core, T, topo):
         def columns(k):
             a, z = 16 * GROUPS[k][0], 16 * GROUPS[k][1]
             o = SL * (len(GROUPS) - k)
+            a -= 1
             scan(at("cum", o + SL * a, o + SL * z), at("wv", SL * (PAD + a), SL * (PAD + z)), at("wv", SL * (PAD + C + a), SL * (PAD + C + z)), A.add, A.add, 16.0)
 
         def steps(k):
@@ -472,91 +499,101 @@ def rank_program(g, core, T, topo):
 
         by_s = list(range(V1, NP)) + list(range(V0 - 1, -1, -1))
         by_v = list(range(V1 - 1, V0 - 1, -1))
-        jobs = [(t, k, p) for t in by_s for k, p in enumerate(parts(t))]
+        jobs = [(t, k, p) for t in by_s for k, p in enumerate(parts(t))] + [(t, 1, parts(t)[1]) for t in WRAPS]
         sign(0, jobs[0])
-        tt(at("lt"), by(at("best"), listR), at("rmax", 0, 512), A.is_gt)
+        tt(at("lt", 0, 272), by(at("best"), listR), at("rmax", 240, 512), A.is_gt)
         compare(by_v[0])
-        scan(at("mid"), at("r20m", 0, 512), at("lt"), A.mult, A.add)
+        scan(at("mid", 0, 272), at("r20m", 0, 272), at("lt", 0, 272), A.mult, A.add)
         compare(by_v[1])
-        for k in range(2):
-            tt(at("vblk", 32 * k, 32 * k + NP), at("mid", 19, 500, 20), at("vcb", 32 * k, 32 * k + NP), A.add)
-            dma("y", kind(k), at("vblk", 32 * k, 32 * k + NP))
         for i, job in enumerate(jobs):
             if i + 1 < len(jobs):
                 sign(i + 1, jobs[i + 1])
             keep(i, job)
+            if i == 1:
+                act(at("midf", 12, NP), at("mid", 19, 260, 20), ACT.Copy)
+                compare(by_v[2])
+                tt(at("vblk"), by(at("midf"), listV), at("vcb", 0, 64), A.add)
+                for k in range(2):
+                    dma("y", kind(k), at("vblk", 32 * k, 32 * k + NP))
         tt(slot(NB, 0, C), by(at("piv"), listP), at("rowz"), A.is_le)
-        for t in by_v[2:]:
+        for t in by_v[3:]:
             compare(t)
         unpack(4, lq, lsc)
-        scan(at("dsum"), at("r16", 0, C), slot(NB, 0, C), A.mult, A.add)
-        if EARLY:
-            columns(0)
-            tally(by_v[0])
-            steps(0)
-            tally(by_v[1])
-            across(256, 416, 0)
-            across(288, 416, 1)
-            sixteen(256, 416, 0)
-            sixteen(288, 416, 1)
-            for t in by_v[2:]:
-                tally(t)
-        else:
-            for t in by_v:
-                tally(t)
-            columns(0)
-        act(at("pq", 2, 4 * NP, 4), at("dsum", 15, C, 16), ACT.Copy)
-        act(at("pq", 4 * V0, 4 * V1, 4), at("junk", 175, 176 * (V1 - V0), 176), ACT.Copy)
+        d = SL * (PAD + C) + NB - SL
+        scan(at("dsum", 8, 208), at("wv", d, d + SL * C, 2 * SL), at("wv", d + SL, d + SL * C, 2 * SL), A.add, A.add, -200.0)
+        HELP = list(range(T1, V1))
+        rest = [t for t in by_v if t not in HELP]
+        for t in rest[:TALLY]:
+            tally(t)
+        columns(0)
+        for t in rest[TALLY:]:
+            tally(t)
+        act(at("pq", 2, 4 * NP, 4), at("dsum", 15, 208, 8), ACT.Copy)
+        line(at("pq", 3, 4 * NP, 4), at("dsum", 7, 200, 8), -1.0)
+        for t in HELP:
+            for k, (a, z, o, s) in enumerate(parts(t)):
+                act(at("sg", 192 * k, 192 * k + z - a), slot(s, a, z), ACT.Copy, at("pq", 4 * t + k, 4 * t + k + 1))
+        act(at("pq", 4 * V0, 4 * T1, 4), at("junk", 175, 176 * (T1 - V0), 176), ACT.Copy)
         act(at("vrow"), by(vrep, listM), ACT.Copy)
         if r == 0:
             first_round_columns()
         columns(1)
-        if not EARLY:
-            steps(0)
+        steps(0)
+        a0, a1 = (EARLY, EARLY + 32) if EARLY else (416, 416)
+        if EARLY:
+            steps(1)
+            across(a0, 416, 0)
+            across(a1, 416, 1)
+            sixteen(a0, 416, 0)
+            sixteen(a1, 416, 1)
         columns(2)
-        steps(1)
-        steps(2)
+        if not EARLY:
+            steps(1)
         scan(at("pp"), at("r4", 0, 128), at("pq"), A.mult, A.add)
-        a0, a1 = (256, 288) if EARLY else (416, 416)
+        steps(2)
         across(0, a0, 0)
         across(0, a1, 1)
-        sixteen(0, a0, 0)
-        sixteen(0, a1, 1)
+        if EARLY:
+            sixteen(0, a0, 0)
+            sixteen(0, a1, 1)
+        else:
+            sixteen(0, 832, 0)
         tt(at("nrk"), by(at("cseg"), listS), at("pp", 3, 128, 4), A.subtract)
         ts(at("rko", 0, NP), at("nrk", 0, NP), -1.0, shifted, A.mult, A.add)
         for b in range(4):
             line(at("tb", C * b, C * b + C), bank(4 + b, C), 0.5)
-        if r == 0:
-            plane(0)
-            plane(1)
+        for b in range(PL if r else 1, 4):
+            plane(b)
         act(at("xa", 0, NP), at("nrk", 0, NP), ACT.Relu, scale=-1000.0, bias=over)
         scatter(at("ew"), at("rko", 0, NP), at("vrow"))
         turn(at("etr", 0, K), at("ew", 0, K))
         turn(at("etr", K, 2 * K), at("ew", 16, K + 16))
         cp(at("lst"), by(at("etr"), listE))
         la, lo, le = at("lst", 0, 10), at("lst", 10, 20), at("lst", 20, 30)
-        for b in range(4):
+        for b in range(3):
             line(at("ah", K * b, K * b + K), by(win(b, C), la), 2.0 ** -6)
-        xa = [at("xa", 32 * i, 32 * i + NP) for i in range(3)]
-        tt(xa[1], xa[0], at("nrk", 0, NP), A.subtract)
-        tt(xa[2], xa[1], at("left", 0, NP), A.min)
-        for b in range(4):
+        ts(at("ah", 3 * K, 4 * K), by(win(3, C), la), 2.0 ** -6, None, A.mult)
+        for b in (0, 3, 1, 2):
             tt(at("zt", b, 4 * K, 4), by(at("tb", C * b, C * b + C), lo), at("ah", K * b, K * b + K), A.add)
         for b in range(4):
             act(at("te", K * b, K * b + K), by(win(b, C), le), ACT.Copy)
+        xa = [at("xa", 32 * i, 32 * i + NP) for i in range(3)]
         quant(at("zq"), at("zsc"), at("zt"))
+        tt(xa[1], xa[0], at("nrk", 0, NP), A.subtract)
+        tt(xa[2], xa[1], at("left", 0, NP), A.min)
         ts(at("xo", 0, NP), xa[2], first, None, A.add)
         for b in range(4):
             mm(4 + b, K, at("wq", 128 * b, 128 * b + 128), at("wsc", 128 * b, 128 * b + 128), at("zq"), at("zsc"))
         for b in range(4):
             tt(at("w32", WW * b, WW * b + K), bank(4 + b, K), at("te", K * b, K * b + K), A.add)
-        for b, a, z, e in ((0, 0, NP, "s"), (3, 0, NP, "v"), (1, 0, NP, "s"), (2, 12, NP, "v"), (2, 0, 12, "s")):
-            o, w = at("xt", 64 * a + b, 64 * z, 4), by(win(b, C + K), at("xo", a, z))
-            if e == "s":
-                line(o, w, 2.0 ** -5)
-            else:
-                ts(o, w, 2.0 ** -5, None, A.mult)
-        quant(at("xq%d" % (r + 1)), at("xs%d" % (r + 1)), at("xt"))
+        for a, z, share in ((CUT, NP, "ssvv"), (0, CUT, "sssv")):
+            for b in (0, 3, 1, 2):
+                o, w = at("xt", 64 * a + b, 64 * z, 4), by(win(b, C + K), at("xo", a, z))
+                if share[b] == "s":
+                    line(o, w, 2.0 ** -5)
+                else:
+                    ts(o, w, 2.0 ** -5, None, A.mult)
+            quant(at("xq%d" % (r + 1), 16 * a, 16 * z), at("xs%d" % (r + 1), 16 * a, 16 * z), at("xt", 64 * a, 64 * z))
 
     xq, xs = "xq%d" % ROUNDS, "xs%d" % ROUNDS
     for h in (1, 0):
@@ -564,13 +601,14 @@ def rank_program(g, core, T, topo):
 
     def scales(k):
         return hbm(T.osc[4 * k:4 * k + 4, :]), (T[xs][32 * k:32 * k + 4, :], at(xs)[1])
-    dma("y", hbm(T.oc[:]), u8(at(xq)))
-    cp(at("yo", 0, 200), bank(0, 200))
+    dma("y", hbm(T.oc[:, 64 * CUT:4 * C]), u8(at(xq, 16 * CUT, C)))
     act(at("yo", 200, C), bank(1, 200), ACT.Copy)
-    dma("y", *scales(0))
-    dma("y", hbm(T.y[:, 0:200]), at("yo", 0, 200))
+    cp(at("yo", 0, 200), bank(0, 200))
     dma("s", hbm(T.y[:, 200:400]), at("yo", 200, C))
-    dma("y", *scales(1))
+    dma("y", hbm(T.oc[:, 0:64 * CUT]), u8(at(xq, 0, 16 * CUT)))
     dma("s", *scales(2))
     dma("s", *scales(3))
+    dma("y", *scales(0))
+    dma("y", *scales(1))
+    dma("y", hbm(T.y[:, 0:200]), at("yo", 0, 200))
     need("g", list(count.items()))

from concourse.mybir import dt, AluOpType, ActivationFunctionType

C, L, K, ROUNDS = 400, 20, 160, 3
MASKS = [1, 2, 3]
NP = 25
NB = 12
V0, V1 = 13, 25
EARLY = 0
WRAPS = []
TALLY = 11
OWN = 1
WIDE = 1
T1 = 23
PL = 3
CUT = 12
MID = (3, 5, 4)
SL = 7
PAD = 160
GROUPS = [(16, 25), (8, 16), (0, 8)]
WW = 576
BIG = 2.0 ** 90
UP = 136.0

F32, BF, F16, I32, U16, X4, U8 = "float32", "bfloat16", "float16", "int32", "uint16", "float8_e4m3fn_x4", "uint8"
SCRATCH = {"ps": ("psum", [128, 4096], F32)}
for _d, _l in (
    (BF, dict(xin=4 * C, uin=512, vin=512, et=516, ones=520, quo=128, qrow=C, pen=C, rst=C, r20m=520, r16=832, r4=C, mjt=200, lt=272, mid=272,
              wv=2 * SL * (PAD + C), dsum=208, junk=176 * 16, sg=4 * 192, cs=432, ctr=832, cseg=960,
              tt=4 * C, w32=4 * WW, tb=4 * C, ah=4 * K, te=4 * K, zt=4 * K, xt=4 * C)),
    (F16, dict(cum=SL * (C + 8))),
    (F32, dict(pc=20, km=12, n16=32, nn=32, left=32, terms=608, tsum=840, r20a=512, sel1=C, sel1h=200, sel0=C, a0=C + 48,
               aexp=512, sums=512, rmax=528, best=32, midf=32, brep=432, btr=800, row=C, rowz=C, piv=C, pq=128, pp=128, nrk=32, seq=32,
               vblk=64, vcb=96, vrep=C, vrow=C, ew=C + 16, etr=2 * K, xa=96, yo=C,
               out0=100, out1=100, out2=100, land0=100, land1=100, land2=100)),
    (I32, dict(pi=1, pb=8, ui=16)),
    (U16, dict(uo=16, co=210, rko=32, lst=32, xo=32)),
    (X4, dict(wq=512, uq=128, urq=256, vq=128, eq=512, zq=K, xq0=C, xq1=C, xq2=C, xq3=C, tq0=C, tq1=C, tq2=C, lq0=C, lq1=C, lq2=C)),
    (U8, dict(wsc=512, usc=128, ursc=256, vsc=128, esc=512, zsc=K, xs0=C, xs1=C, xs2=C, xs3=C, ts0=C, ts1=C, ts2=C, ls0=C, ls1=C, ls2=C)),
):
    for _n, _w in _l.items():
        SCRATCH[_n] = ("sbuf", [128, _w], _d)
SEMAPHORES = (["cv", "cs", "ct", "cg", "sent"] + ["d%d" % _i for _i in range(24)]
              + ["arrs%d" % _r for _r in range(ROUNDS)] + ["arrc%d" % _r for _r in range(ROUNDS)])

A = AluOpType
ACT = ActivationFunctionType


def rank_program(g, core, T, topo):
    rank = T.rank_of(core)
    if rank is None:
        return
    V, S, PE = g.vector, g.scalar, g.tensor
    queue = {"v": V, "s": S, "t": PE, "g": g, "y": g.sync}
    own = {"v": "cv", "s": "cs", "t": "ct", "g": "cg"}
    count = {}
    waited = {e: {} for e in queue}
    touched = {}
    ndma = [0]

    def bits(a, z, step=1):
        n = (z - a + step - 1) // step
        return ((1 << (n * step)) - 1) // ((1 << step) - 1) << a

    def at(name, a=0, z=None, step=1):
        if z is None:
            z = SCRATCH[name][1][1]
        return (T[name][:, a:z:step], [(name, bits(a, z, step))])

    def by(win, off):
        return (win[0].indirect(off[0]), win[1] + off[1])

    def words(view):
        return (view[0].bitcast(dt.uint32), view[1])

    def u8(view):
        return (view[0].bitcast(dt.uint8), view[1])

    def bank(k, n, a=0):
        return (T.ps[:, 512 * k + a:512 * k + a + n], [("bank%d" % k, 1)])

    def hbm(ap):
        return (ap, [])

    def ap(x):
        return x[0] if isinstance(x, tuple) else x

    def need(e, deps):
        top = {}
        for s, n in deps:
            top[s] = max(top.get(s, 0), n)
        for s, n in top.items():
            if waited[e].get(s, 0) < n:
                queue[e].wait_ge(T.sem[s], n)
                waited[e][s] = n

    def order(e, R, W):
        deps = []
        for name, m in R:
            deps += [x[1] for x in touched.get(name, []) if x[0] & m and (x[2] or (name[:4] == "bank" and x[1][0] != own.get(e)))]
        for name, m in W:
            deps += [x[1] for x in touched.get(name, []) if x[0] & m]
        need(e, deps)

    def done(mark, R, W):
        for name, m in W:
            touched[name] = [[x[0] & ~m, x[1], x[2]] for x in touched.get(name, []) if x[0] & ~m] + [[m, mark, True]]
        for name, m in R:
            touched.setdefault(name, []).append([m, mark, False])

    def regions(views):
        return [r for v in views if isinstance(v, tuple) for r in v[1]]

    def op(e, call, outs, ins):
        R, W = regions(ins), regions(outs)
        order(e, R, W)
        s = own[e]
        call().then_inc(T.sem[s], 1)
        count[s] = count.get(s, 0) + 1
        done((s, count[s]), R, W)

    def dma(e, out, in_, after=()):
        R, W = regions([in_] + list(after)), regions([out])
        order(e, R, W)
        s = "d%d" % ndma[0]
        ndma[0] += 1
        queue[e].dma_start(out[0], in_[0]).then_inc(T.sem[s], 16)
        count[s] = 16
        done((s, 16), R, W)

    def engines_of(m):
        return bin(m).count("1")

    def send(dst, out, in_, sem, m):
        order("g", in_[1], [])
        rid, pid = topo.addr(dst)[:2]
        g.remote_dma(out[0], in_[0], T.sem[sem], T.sem.sent, pid, rid, m)
        count["sent"] = count.get("sent", 0) + engines_of(m)
        count[sem] = count.get(sem, 0) + engines_of(m)

    def arrives(sem, *views):
        done((sem, count[sem]), [], regions(views))

    def ts(out, in0, s1, s2, o0, o1=None):
        if o1 is None:
            op("v", lambda: V.tensor_scalar(out[0], in0[0], ap(s1), None, o0), [out], [in0, s1])
        else:
            op("v", lambda: V.tensor_scalar(out[0], in0[0], ap(s1), ap(s2), o0, o1), [out], [in0, s1, s2])

    def tt(out, in0, in1, o):
        op("v", lambda: V.tensor_tensor(out[0], in0[0], in1[0], o), [out], [in0, in1])

    def cp(out, in_):
        op("v", lambda: V.tensor_copy(out[0], in_[0]), [out], [in_])

    def scatter(win, off, in_):
        op("v", lambda: V.tensor_copy(win[0].indirect(off[0]), in_[0]), [win], [off, in_])

    def scan(out, d0, d1, o0, o1, first=0.0):
        op("v", lambda: V.tensor_tensor_scan(out[0], d0[0], d1[0], ap(first), o0, o1), [out], [d0, d1, first])

    def turn(out, in_):
        op("v", lambda: V.transpose(out[0], in_[0]), [out], [in_])

    def quant(codes, plane, tile):
        op("v", lambda: V.quantize_mx(codes[0], plane[0], tile[0]), [codes, plane], [tile])

    def mset(out, c):
        op("v", lambda: V.memset(out[0], c), [out], [])

    def act(out, in_, f, total=None, **kw):
        k = {n: ap(x) for n, x in kw.items()}
        if total:
            k["accum_out"] = total[0]
        op("s", lambda: S.activation(out[0], in_[0], f, **k), [out, total], [in_] + list(kw.values()))

    def line(out, in_, scale, bias=0.0):
        act(out, in_, ACT.Identity, scale=scale, bias=bias)

    def iota(out, pattern, base=0, cm=0, small=True):
        if small:
            op("g", lambda: g.iota(out[0], pattern, base, cm, allow_small_or_imprecise_dtypes=True), [out], [])
        else:
            op("g", lambda: g.iota(out[0], pattern, base, cm), [out], [])

    def ones_where(name, pattern, compare, base=0, cm=0, a=0, n=None):
        n = n or SCRATCH[name][1][1]
        out, one = at(name, a, a + n), at("ones", 0, n)
        op("g", lambda: g.affine_select(out[0], one[0], pattern, compare, 0.0, base, cm), [out], [one])

    def mm(k, n, lq, ls, rq, rs):
        out = bank(k, n)
        op("t", lambda: PE.matmul_mx(out[0], lq[0], ls[0], rq[0], rs[0], True, True), [out], [lq, ls, rq, rs])

    def col(i, n=1):
        return at("pc", i, i + n)

    partners = [T.cores[rank ^ s] for s in MASKS]
    common = topo.mask(core, partners[0])
    for d in partners:
        common &= topo.mask(core, d)

    dma("s", at("uin"), hbm(T.u[:]))
    dma("y", at("xin", 800, 1600), hbm(T.x[:, 800:1600]))
    dma("s", at("xin", 0, 800), hbm(T.x[:, 0:800]))

    LA, LB, LB2, LC, LN, LM, LS, LE, LR, LV, LP = 0, 32, 48, 66, 96, 122, 148, 150, 152, 170, 174
    listA, listB, listC = at("co", LA, LA + 32), [at("co", LB, LB + 15), at("co", LB2, LB2 + 17)], [at("co", LC, LC + 13), at("co", LC + 16, LC + 30)]
    listN, listM, listS, listE, listR, listV, listP = [at("co", a, a + n) for a, n in ((LN, NP), (LM, NP), (LS, 2), (LE, 2), (LR, 17), (LV, 4), (LP, NP))]

    def term(a, n, k):
        return at("terms", 4 * a + k, 4 * (a + n), 4)

    def nn(a, z):
        return at("nn", a, z)

    def f20(a, z):
        return at("quo", a, z)

    def f100(a, z):
        return at("quo", 32 + a, 32 + z)

    def f5(a, z):
        return at("quo", 64 + a, 64 + z)

    q, h16, iq, jq, odd, par, flip, i100, j100, ij, first, shifted, over, even, nq, nqh = [col(i) for i in range(16)]
    k4 = at("km", 0, 4)
    iota(at("pi"), [[0, 1]], 0, 1, False)
    iota(at("n16"), [[16, 32]])
    iota(at("ui"), [[1, 2], [16, 8]], small=False)
    iota(k4, [[1, 4]])
    mset(at("ones"), 1.0)
    mset(at("terms", 0, 4 * LC), 0.0)
    ones_where("et", [[1, 516]], A.is_equal, -3, -4)
    ones_where("r4", [[0, 100], [1, 4]], A.not_equal)
    iota(at("seq", 0, 16), [[L, 8], [6 * L, 2]], -1)
    iota(at("seq", 16, 32), [[L, 8], [7 * L, 2]], -1)
    ones_where("r20m", [[0, 26], [1, 20]], A.not_equal)
    iota(at("tsum", 4 * LP + 3, 800, 4), [[16, 26]], 15)
    iota(at("a0", C, C + 48), [[0, 48]])
    ts(at("pb", 0, 1), at("pi"), 15, None, A.bitwise_and)
    ts(at("pb", 1, 2), at("pi"), 16, None, A.bitwise_and)
    ts(at("pb", 2, 3), at("pi"), 2, 3, A.logical_shift_right, A.bitwise_and)
    ts(at("pb", 3, 4), at("pi"), 3, None, A.bitwise_and)
    ts(at("pb", 4, 5), at("pi"), 4, 1, A.logical_shift_right, A.bitwise_and)
    ts(at("pb", 5, 6), at("pi"), 1, None, A.bitwise_and)
    cp(at("uo"), at("ui"))
    cp(col(0, 6), at("pb", 0, 6))
    mset(at("terms", 4 * LC, 4 * LR), 0.0)
    ts(at("km", 8, 12), k4, jq, None, A.is_equal)
    ts(at("km", 4, 8), k4, iq, None, A.is_equal)
    ts(flip, odd, par, 432.0, A.not_equal, A.mult)
    for k in range(2):
        ts(at("mjt", 100 * k, 100 * k + 100), at("ones", 0, 100), at("km", 10 + k, 11 + k), None, A.mult)
    line(at("nn"), at("n16"), 1.0, q)
    line(col(7, 2), col(2, 2), 5.0 * L)
    line(first, q, -1.0, 16.0 * NB + 15)
    line(f20(0, 32), at("nn"), 1.0 / 20, UP - 0.475)
    line(f100(0, 32), at("nn"), 1.0 / 100, UP - 0.495)
    line(term(LA, 32, 0), at("nn"), 4.0, 3.0)
    line(term(LB, 16, 0), nn(0, 16), 1.0, 100 * UP)
    line(term(LB2, 17, 0), nn(15, 32), 1.0, 100 * UP)
    line(term(LA, 32, 1), f20(0, 32), -80.0)
    line(term(LA, 32, 2), f100(0, 32), 80.0)
    line(term(LB, 16, 1), f100(0, 16), -100.0)
    line(term(LB2, 17, 1), f100(15, 32), -100.0)
    line(f5(0, 32), at("nn"), 1.0 / 5, UP - 0.4)
    quant(at("uq"), at("usc"), at("uin"))
    cp(words(at("urq", 128, 256)), by(words(at("uq")), at("uo", 8, 16)))
    act(at("ursc", 128, 256), by(at("usc"), at("uo", 8, 16)), ACT.Copy)
    for a in (200, 0):
        quant(at("xq0", a, a + 200), at("xs0", a, a + 200), at("xin", 4 * a, 4 * a + 800))
    cp(words(at("urq", 0, 128)), by(words(at("uq")), at("uo", 0, 8)))
    act(at("ursc", 0, 128), by(at("usc"), at("uo", 0, 8)), ACT.Copy)
    ts(even, odd, -1.0, 1.0, A.mult, A.add)
    ts(nq, q, -BIG, None, A.mult)
    ts(nqh, q, 0.5, -BIG, A.add, A.mult)
    ts(ij, jq, 5.0, i100, A.mult, A.add)

    def kind(k):
        return (T.vrep[k:128:16, :], [("vrep%d" % k, 1)])
    vrep = (T.vrep[:], [("vrep%d" % k, 1) for k in range(4)])

    def zeros(*views):
        for name, a, z in views:
            iota(at(name, a, z), [[0, z - a]])

    def lists(a, z, upto):
        scan(at("tsum", 4 * a, 4 * z), at("r4", 0, 4 * (z - a)), at("terms", 4 * a, 4 * z), A.mult, A.add)
        cp(at("co", a, upto), at("tsum", 4 * a + 3, 4 * upto, 4))

    def after_first_scores():
        iota(at("qrow"), [[0, 25], [1, 16]])
        zeros(("rmax", 512, 528), ("best", NP, 32))
        iota(at("vcb", 0, 25), [[L, 5], [0, 5]])
        iota(at("vcb", 32, 57), [[0, 5], [L, 5]])
        iota(at("vcb", 64, 89), [[L, 5], [1, 5]])
        for b in range(4):
            quant(at("eq", 128 * b, 128 * b + 128), at("esc", 128 * b, 128 * b + 128), at("et", 3 - b, 515 - b))
        lists(0, LC, LC)

    def later_terms():
        line(term(LN, 26, 0), nn(0, 26), 32.0, h16)
        line(term(LN, 26, 1), f20(0, 26), 156.0, UP * 799)
        line(term(LN, 26, 2), f100(0, 26), -796.0)
        line(term(LN, 26, 3), f5(0, 26), -159.0)
        line(term(LM, 26, 0), nn(0, 26), 1.0)
        line(term(LM, 26, 1), f20(0, 26), -95.0)
        line(term(LM, 26, 2), f100(0, 26), 75.0)
        line(term(LM, 26, 3), f5(0, 26), 20.0)
        line(at("quo", 96, 98), nn(0, 2), 1.0 / 2, UP - 0.25)
        line(at("quo", 98, 100), nn(0, 2), 1.0 / 10, UP - 0.45)
        line(term(LC, 30, 0), at("seq", 2, 32), even)
        line(term(LC, 30, 1), at("seq", 1, 31), odd)
        line(term(LS, 2, 0), nn(0, 2), 16.0, flip)
        line(term(LS, 2, 1), nn(0, 2), 0.0, 15.0)
        line(term(LE, 2, 0), nn(0, 2), 160.0, h16)
        line(term(LE, 2, 1), at("quo", 96, 98), -288.0, UP * 447)
        line(term(LE, 2, 2), at("quo", 98, 100), -159.0)
        line(at("tsum", 4 * LR + 3, 4 * LV, 4), f20(15, 33), 1.0, -UP)
        for a in (LV, LV + 2):
            line(at("tsum", 4 * a + 3, 4 * a + 8, 4), nn(0, 2), 1.0)

    def after_first_codes():
        zeros(("vcb", NP, 32), ("vcb", 32 + NP, 64))
        iota(vrep, [[0, C]])
        zeros(("midf", NP, 32))
        iota(at("dsum", 7, 8), [[0, 1]], -200)
        for a in (0, 416):
            ones_where("r16", [[0, 26], [1, 16]], A.not_equal, a=a, n=416)
        iota(slot(2 * SL - 1, 0, C), [[0, C]])
        zeros(("pq", 0, 128))
        for k in range(4, -1, -1):
            iota(slot(SL + k, C, C + 32 * (k + 1)), [[0, 32 * (k + 1)]])
        for k in range(4, -1, -1):
            iota(slot(k, -32 * (5 - k), 0), [[0, 32 * (5 - k)]])
        zeros(("cs", 0, 16), ("cs", 416, 432), ("ew", 0, 16), ("cseg", 832, 960))
        zeros(("wv", SL * (PAD - 1), SL * PAD))

    def first_round_masks():
        act(at("pen"), at("qrow"), ACT.Relu, scale=BIG, bias=nq)
        line(at("rst"), at("qrow"), BIG, nqh)
        line(at("vcb", 0, NP), at("vcb", 0, NP), 1.0, i100)
        line(at("vcb", 32, 32 + NP), at("vcb", 32, 32 + NP), 1.0, j100)
        line(at("vcb", 64, 64 + NP), at("vcb", 64, 64 + NP), 1.0, ij)
        dma("y", kind(2), at("vcb", 64, 64 + NP))

    def first_round_columns():
        line(shifted, first, 1.0, h16)
        line(over, first, 1000.0, -1000.0 * (K - 1))
        line(at("left", 0, NP), at("n16", 0, NP), 1.0, K - 16.0 * NB - 15)
        line(at("left", 0, NP), at("left", 0, NP), 1.0, q)
        line(at("left", 0, NP), at("left", 0, NP), 1.0, q)

    def slot(s, a, z):
        o = SL * (PAD + (s // SL) * C) + s % SL
        return at("wv", o + SL * a, o + SL * (z - 1) + 1, SL)

    def ends(k, a, z):
        o = SL * (len(GROUPS) - k) + SL - 1
        return at("cum", o + SL * a, o + SL * (z - 1) + 1, SL)

    def win(b, n):
        return at("w32", WW * b + C + K - n, WW * b + C + K)

    def plane(b):
        line(win(b, C), bank(b, C), 32.0)

    def unpack(k, codes, scales):
        for b in range(4):
            mm(k + b, C, at("eq", 128 * b, 128 * b + 128), at("esc", 128 * b, 128 * b + 128), codes, scales)

    for r in range(ROUNDS):
        dst = partners[r]
        wide = topo.mask(core, dst)
        xq, xs = "xq%d" % r, "xs%d" % r
        out, land = at("out%d" % r), at("land%d" % r)
        tq, tsc, lq, lsc = at("tq%d" % r), at("ts%d" % r), at("lq%d" % r), at("ls%d" % r)

        for h in (1, 0):
            mm(4 + h, 200, at("urq", 128, 256), at("ursc", 128, 256), at(xq, 200 * h, 200 * h + 200), at(xs, 200 * h, 200 * h + 200))
        for k in range(2):
            line(at("sel1", 100 * k, 100 + 100 * k), bank(4, 100, 100 * k), at("km", 8 + k, 9 + k))
        tt(at("sel1", 200, C), bank(5, 200), at("mjt"), A.mult)
        tt(at("sel1h", 0, 100), at("sel1", 200, 300), at("sel1", 300, C), A.add)
        tt(at("sel1h", 100, 200), at("sel1h", 0, 100), at("sel1", 0, 100), A.add)
        tt(out, at("sel1h", 100, 200), at("sel1", 100, 200), A.add)
        send(dst, land, out, "arrs%d" % r, wide if WIDE else common)
        arrives("arrs%d" % r, land)

        mm(6, C, at("urq", 0, 128), at("ursc", 0, 128), at(xq), at(xs))
        if r == 0:
            after_first_scores()
        unpack(0, at(xq), at(xs))
        for k in range(4):
            line(at("sel0", k, C, 4), bank(6, 100, 100 * k), at("km", 4 + k, 5 + k))
        scan(at("a0", 0, C), at("r4"), at("sel0"), A.mult, A.add)
        if r == 0:
            later_terms()
        act(at("tt", 0, 4 * C, 4), bank(0, C), ACT.Copy)
        act(at("aexp"), by(at("a0"), listA), ACT.Copy)
        if r == 0:
            line(at("r20a"), at("r20m", 0, 512), BIG, -BIG)
            lists(LC, LR, 200)
        for b in range(1, 4):
            cp(at("tt", b, 4 * C, 4), bank(b, C))
        quant(tq, tsc, at("tt"))
        send(dst, u8(lq), u8(tq), "arrc%d" % r, wide)
        send(dst, lsc, tsc, "arrc%d" % r, wide)
        arrives("arrc%d" % r, lq, lsc)
        if r == 0:
            after_first_codes()
            first_round_masks()
            dma("y", u8(at("wq")), hbm(T.wc[:]), [land])
            dma("y", at("wsc"), hbm(T.ws[:]))
            dma("y", at("vin"), hbm(T.v[:]))
        for b in range(PL if r else 1):
            plane(b)
        if r == 1:
            quant(at("vq"), at("vsc"), at("vin"))

        def middles(a, n):
            for u in range(a, a + n):
                act(at("sg", L * u, L * u + L), at("rmax", L * u, L * u + L), ACT.Sign, at("midf", u, u + 1), scale=-1.0,
                    bias=at("rmax", L * u + L - 1, L * u + L))

        for k, (a, z, o, n) in enumerate(((0, 240, 0, 208), (240, 512, 208, 224))):
            tt(at("sums", a, z), by(land, listB[k]), at("aexp", a, z), A.add)
            scan(at("rmax", a, z), at("r20a", a, z), at("sums", a, z), A.add, A.max)
            act(at("brep", o, o + n), by(at("rmax", a, z + 16 * k), listC[k]), ACT.Copy)
            if k == 0:
                middles(0, MID[0])
        act(at("best", 0, NP), at("rmax", 19, 500, 20), ACT.Copy)
        turn(at("btr", 0, 192), at("brep", 0, 192))
        turn(at("btr", 192, 384), at("brep", 16, 208))
        turn(at("btr", 384, 608), at("brep", 208, 432))
        turn(at("btr", 608, 800), at("brep", 224, 416))
        middles(MID[0], MID[1])
        act(at("row"), by(at("btr"), listN), ACT.Copy)
        tt(at("rowz"), by(at("btr"), listN), at("pen"), A.subtract)
        middles(MID[0] + MID[1], MID[2])
        scan(at("piv"), at("rst"), at("rowz"), A.min, A.max)

        def pivot(t):
            return at("piv", 16 * t + 15, 16 * t + 16)

        def parts(t):
            a, z = 16 * (t + 1), 16 * (t + 1 + NB)
            return ([(a, min(z, C), A.is_gt, t % NB)] if a < C else []) + ([(0, z - C, A.is_ge, t - NB - 1)] if z > C else [])

        def sign(i, job):
            t, k, (a, z, o, s) = job
            act(at("sg", 192 * (i % 4), 192 * (i % 4) + z - a), at("row", a, z), ACT.Sign, bias=pivot(t), scale=-1.0)

        def keep(i, job):
            t, k, (a, z, o, s) = job
            signs, total = at("sg", 192 * (i % 4), 192 * (i % 4) + z - a), at("pq", 4 * t + k, 4 * t + k + 1)
            if o == A.is_gt:
                act(slot(s, a, z), signs, ACT.Relu, total, scale=-1.0)
            else:
                act(slot(s, a, z), signs, ACT.Sign, total, scale=-1.0, bias=1.0)

        def mine(t):
            return parts(t)[:1] if t in WRAPS else parts(t)

        def compare(t):
            for a, z, o, s in mine(t):
                ts(slot(s, a, z), at("row", a, z), pivot(t), None, o)

        def tally(t):
            p = mine(t)
            if len(p) == 1:
                a, z, o, s = p[0]
                n = (z - a) // 2
                d0, d1 = slot(s, a, a + n), slot(s, a + n, z)
            else:
                n = max(p[0][1] - p[0][0], p[1][1])
                d0, d1 = slot(p[0][3], p[0][0], p[0][0] + n), slot(p[1][3], p[1][1] - n, p[1][1])
            e = 176 * (t - V0 + 1)
            scan(at("junk", e - n, e), d0, d1, A.add, A.add)

        def columns(k):
            a, z = 16 * GROUPS[k][0], 16 * GROUPS[k][1]
            o = SL * (len(GROUPS) - k)
            a -= 1
            scan(at("cum", o + SL * a, o + SL * z), at("wv", SL * (PAD + a), SL * (PAD + z)), at("wv", SL * (PAD + C + a), SL * (PAD + C + z)), A.add, A.add, 16.0)

        def steps(k):
            a, z = 16 * GROUPS[k][0], 16 * GROUPS[k][1]
            scan(at("cs", 16 + a, 16 + z), ends(k, a, z), ends(k, a - 1, z - 1), A.max, A.subtract)

        def across(a, z, shift):
            o = 416 * shift
            turn(at("ctr", o + a, o + z), at("cs", 16 - 16 * shift + a, 16 - 16 * shift + z))

        def sixteen(a, z, shift):
            o = 416 * shift
            scan(at("cseg", o + a, o + z), at("r16", 0, z - a), at("ctr", o + a, o + z), A.mult, A.add)

        by_s = list(range(V1, NP)) + list(range(V0 - 1, -1, -1))
        by_v = list(range(V1 - 1, V0 - 1, -1))
        jobs = [(t, k, p) for t in by_s for k, p in enumerate(parts(t))] + [(t, 1, parts(t)[1]) for t in WRAPS]
        sign(0, jobs[0])
        tt(at("lt", 0, 272), by(at("best"), listR), at("rmax", 240, 512), A.is_gt)
        compare(by_v[0])
        scan(at("mid", 0, 272), at("r20m", 0, 272), at("lt", 0, 272), A.mult, A.add)
        compare(by_v[1])
        for i, job in enumerate(jobs):
            if i + 1 < len(jobs):
                sign(i + 1, jobs[i + 1])
            keep(i, job)
            if i == 1:
                act(at("midf", 12, NP), at("mid", 19, 260, 20), ACT.Copy)
                compare(by_v[2])
                tt(at("vblk"), by(at("midf"), listV), at("vcb", 0, 64), A.add)
                for k in range(2):
                    dma("y", kind(k), at("vblk", 32 * k, 32 * k + NP))
        tt(slot(NB, 0, C), by(at("piv"), listP), at("rowz"), A.is_le)
        for t in by_v[3:]:
            compare(t)
        unpack(4, lq, lsc)
        d = SL * (PAD + C) + NB - SL
        scan(at("dsum", 8, 208), at("wv", d, d + SL * C, 2 * SL), at("wv", d + SL, d + SL * C, 2 * SL), A.add, A.add, -200.0)
        HELP = list(range(T1, V1))
        rest = [t for t in by_v if t not in HELP]
        for t in rest[:TALLY]:
            tally(t)
        columns(0)
        for t in rest[TALLY:]:
            tally(t)
        act(at("pq", 2, 4 * NP, 4), at("dsum", 15, 208, 8), ACT.Copy)
        line(at("pq", 3, 4 * NP, 4), at("dsum", 7, 200, 8), -1.0)
        for t in HELP:
            for k, (a, z, o, s) in enumerate(parts(t)):
                act(at("sg", 192 * k, 192 * k + z - a), slot(s, a, z), ACT.Copy, at("pq", 4 * t + k, 4 * t + k + 1))
        act(at("pq", 4 * V0, 4 * T1, 4), at("junk", 175, 176 * (T1 - V0), 176), ACT.Copy)
        act(at("vrow"), by(vrep, listM), ACT.Copy)
        if r == 0:
            first_round_columns()
        columns(1)
        steps(0)
        a0, a1 = (EARLY, EARLY + 32) if EARLY else (416, 416)
        if EARLY:
            steps(1)
            across(a0, 416, 0)
            across(a1, 416, 1)
            sixteen(a0, 416, 0)
            sixteen(a1, 416, 1)
        columns(2)
        if not EARLY:
            steps(1)
        scan(at("pp"), at("r4", 0, 128), at("pq"), A.mult, A.add)
        steps(2)
        across(0, a0, 0)
        across(0, a1, 1)
        if EARLY:
            sixteen(0, a0, 0)
            sixteen(0, a1, 1)
        else:
            sixteen(0, 832, 0)
        tt(at("nrk"), by(at("cseg"), listS), at("pp", 3, 128, 4), A.subtract)
        ts(at("rko", 0, NP), at("nrk", 0, NP), -1.0, shifted, A.mult, A.add)
        for b in range(4):
            line(at("tb", C * b, C * b + C), bank(4 + b, C), 0.5)
        for b in range(PL if r else 1, 4):
            plane(b)
        act(at("xa", 0, NP), at("nrk", 0, NP), ACT.Relu, scale=-1000.0, bias=over)
        scatter(at("ew"), at("rko", 0, NP), at("vrow"))
        turn(at("etr", 0, K), at("ew", 0, K))
        turn(at("etr", K, 2 * K), at("ew", 16, K + 16))
        cp(at("lst"), by(at("etr"), listE))
        la, lo, le = at("lst", 0, 10), at("lst", 10, 20), at("lst", 20, 30)
        for b in range(3):
            line(at("ah", K * b, K * b + K), by(win(b, C), la), 2.0 ** -6)
        ts(at("ah", 3 * K, 4 * K), by(win(3, C), la), 2.0 ** -6, None, A.mult)
        for b in (0, 3, 1, 2):
            tt(at("zt", b, 4 * K, 4), by(at("tb", C * b, C * b + C), lo), at("ah", K * b, K * b + K), A.add)
        for b in range(4):
            act(at("te", K * b, K * b + K), by(win(b, C), le), ACT.Copy)
        xa = [at("xa", 32 * i, 32 * i + NP) for i in range(3)]
        quant(at("zq"), at("zsc"), at("zt"))
        tt(xa[1], xa[0], at("nrk", 0, NP), A.subtract)
        tt(xa[2], xa[1], at("left", 0, NP), A.min)
        ts(at("xo", 0, NP), xa[2], first, None, A.add)
        for b in range(4):
            mm(4 + b, K, at("wq", 128 * b, 128 * b + 128), at("wsc", 128 * b, 128 * b + 128), at("zq"), at("zsc"))
        for b in range(4):
            tt(at("w32", WW * b, WW * b + K), bank(4 + b, K), at("te", K * b, K * b + K), A.add)
        for a, z, share in ((CUT, NP, "ssvv"), (0, CUT, "sssv")):
            for b in (0, 3, 1, 2):
                o, w = at("xt", 64 * a + b, 64 * z, 4), by(win(b, C + K), at("xo", a, z))
                if share[b] == "s":
                    line(o, w, 2.0 ** -5)
                else:
                    ts(o, w, 2.0 ** -5, None, A.mult)
            quant(at("xq%d" % (r + 1), 16 * a, 16 * z), at("xs%d" % (r + 1), 16 * a, 16 * z), at("xt", 64 * a, 64 * z))

    xq, xs = "xq%d" % ROUNDS, "xs%d" % ROUNDS
    for h in (1, 0):
        mm(h, 200, at("vq"), at("vsc"), at(xq, 200 * h, 200 * h + 200), at(xs, 200 * h, 200 * h + 200))

    def scales(k):
        return hbm(T.osc[4 * k:4 * k + 4, :]), (T[xs][32 * k:32 * k + 4, :], at(xs)[1])
    dma("y", hbm(T.oc[:, 64 * CUT:4 * C]), u8(at(xq, 16 * CUT, C)))
    act(at("yo", 200, C), bank(1, 200), ACT.Copy)
    cp(at("yo", 0, 200), bank(0, 200))
    dma("s", hbm(T.y[:, 200:400]), at("yo", 200, C))
    dma("y", hbm(T.oc[:, 0:64 * CUT]), u8(at(xq, 0, 16 * CUT)))
    dma("s", *scales(2))
    dma("s", *scales(3))
    dma("y", *scales(0))
    dma("y", *scales(1))
    dma("y", hbm(T.y[:, 0:200]), at("yo", 0, 200))
    need("g", list(count.items()))
